import numpy as np, ml_dtypes
CORES = [2,7,18,23,34]
N = 5
BF = ml_dtypes.bfloat16
def gentries(a):
    return np.ascontiguousarray(a.reshape(8, 16, -1).transpose(0, 2, 1)).reshape(8, -1)
def gtable(e):
    e = np.asarray(e); return np.ascontiguousarray(e.reshape(8, -1, 16).transpose(0, 2, 1)).reshape(128, -1).astype(np.int32)
W, L, P, T = 2048, 128, 32, 6
def place(z, e, kap):
    return ((z * (2 * e + 1)[..., None] >> 5) + z + kap) & (W - 1)
def parts(rng):
    low = rng.random((N, 8, 1, W)) < rng.choice(np.array([0.01, 0.03, 0.06, 0.15, 0.5]), (N, 8, 1, 1))
    x = np.where(low, rng.integers(0, 256, (N, 8, 16, W)), rng.integers(64, 256, (N, 8, 16, W)))
    c = rng.integers(0, W, (N, 8, L, 16)); o = rng.integers(0, W, (N, 8, L, P))
    d = np.where(rng.random((N, 8, 1, L)) < 0.5, rng.integers(1, 49, (N, 8, 16, L)), rng.integers(1, 256, (N, 8, 16, L)))
    return x, c, o, d, rng.integers(0, 16, (N, 8, 16, 1))
def pack(x, c, o, d, w):
    return {"xt": np.ascontiguousarray(x.reshape(N, 128, W)).astype(np.float32).astype(BF), "pk": np.stack([gtable(a.reshape(8, -1)) for a in c]), "po": np.stack([gtable(a.reshape(8, -1)) for a in o]),
            "dm": np.ascontiguousarray(d.reshape(N, 128, L)).astype(np.int32), "wt": np.ascontiguousarray(w.reshape(N, 128, 1)).astype(np.int32)}
def setup_inputs(rng):
    return pack(*parts(rng))
def setup_inputs_ties(rng):
    x, c, o, d, w = parts(rng)
    v = rng.integers(8, 200, (N, 8, 16, 1))
    x = v + np.where(rng.random((N, 8, 1, W)) < 0.75, rng.integers(-1, 2, (N, 8, 1, W)), rng.integers(-1, 2, (N, 8, 16, W)))
    d = v + rng.integers(-1, 2, (N, 8, 16, L))
    few = rng.integers(0, W, 8); few[0] = 0; few[7] = W - 1
    c[:, 1::2] = few[rng.integers(0, 8, (N, 4, L, 16))]; o[:, 1::2] = few[rng.integers(0, 8, (N, 4, L, P))]
    return pack(x, c, o, d, w)
def setup_inputs_corners(rng):
    x, c, o, d, w = parts(rng)
    d = rng.choice(np.array([1, 2, 4, 5, 6, 8, 9, 10, 128, 246, 247, 248, 251, 252, 255]), (N, 8, 16, L))
    d[:, :, :, :8] = 1; d[:, :, :, L - 8:] = 255
    x[:, 0] = x[:, 0, :, :1]
    c[:, 1] = c[:, 1, :, :1]; o[:, 1] = o[:, 1, :, :1]
    o[:, 2] = np.concatenate([c[:, 2, :, ::-1]] * (P // 16), axis=2)
    w[:, 3] = 0; w[:, 4] = 15; w[:, 5] = 0; w[:, 5, 15] = rng.integers(1, 16, (N, 1))
    x[:, 6] = 255 * rng.integers(0, 2, (N, 1, W))
    x[:, 7] = rng.integers(0, 256, (N, 16, W)); c[:, 7] = (W - 1) * rng.integers(0, 2, (N, L, 16)); o[:, 7] = (W - 1) * rng.integers(0, 2, (N, L, P))
    q = int(rng.integers(0, N)); x[q] = x[q, :, :, :1]
    return pack(x, c, o, d, w)
def setup_inputs_ends(rng):
    kind = rng.integers(0, 4, (N, 8, 1, W)); hole = rng.integers(0, 16, (N, 8, 1, W))
    x = np.where(kind == 0, 0, np.where(kind == 1, 1, np.where(kind == 2, rng.integers(0, 2, (N, 8, 16, W)), np.arange(16).reshape(16, 1) != hole)))
    w = rng.integers(0, 2, (N, 8, 16, 1)); w[:, 6] = 0; w[:, 7] = 1; w = 15 * w
    kd = rng.integers(0, 4, (N, 8, 1, L)); d = np.where(kd == 0, 0, np.where(kd == 1, 1, rng.integers(0, 2, (N, 8, 16, L))))
    d[:, :, :, L - 1] = 1; d[:, :, :, L - 2] = 0; d = 1 + 254 * d
    c = (W - 1) * rng.integers(0, 2, (N, 8, L, 16)); o = (W - 1) * rng.integers(0, 2, (N, 8, L, P))
    c[:, :, L - 2:] = 0; c[:, :, L - 2:, 15] = W - 1; c[:, :, L - 1, 2] = W - 1
    o[:, :, L - 2:] = W - 1; o[:, :, L - 2:, P - 1] = 0; o[:, :, L - 1, 1] = 0
    c[0, :, :, 7] = W - 1; o[0, :, :, P - 1] = 0; c[0, 3, 5] = 0
    c[N - 1, :, :, 15] = W - 1; o[N - 1, :, :, P - 1] = 0
    m = rng.random((8, L, 1)) < 0.5; c[1] = np.where(m, 0, W - 1); o[1] = np.where(m, o[1], W - 1)
    e = np.add.reduce(w * d, axis=2) & 1023
    p = place(np.full((N, 8, L, 1), W - 1), e, 0)[..., 0]
    tail = int(np.argmax(place(np.arange(W)[None, :], np.zeros(1, np.int64), 0)[0]))
    for q in (0, 1, N - 1):
        for g in range(8): x[q, g][:, p[q, g]] = 1
        x[q, :, :, 0] = 0
    for q in (0, N - 1):
        c[q, 6, L - 2:, 15] = tail; x[q, 6, :, W - 1] = 1
    return pack(255 * x, c, o, d, w)
def setup_inputs_lull(rng):
    x, c, o, d, w = parts(rng)
    q = int(rng.integers(0, N)); p = (q - 1) % N
    x[q] = np.maximum(x[q], 1); x[:, :, :, :32] = 255; x[p, :, :, :32] = 0; x[q, :, :, :32] = 0
    c[p] = 0; o[q, :, :, P - 2:] = 0; o[q] = rng.permuted(o[q], axis=2)
    still = rng.permutation(8 * L)[:int(rng.integers(1, 32))]; c[q, still // L, still % L] = 0
    return pack(x, c, o, d, w)
def setup_inputs_spread(rng):
    x = np.minimum((np.exp2(8 * rng.random((N, 8, 1, W))) * (0.5 + 0.5 * rng.random((N, 8, 16, W)))).astype(np.int64), 255) * (rng.random((N, 8, 1, W)) > 0.0625)
    c = np.minimum((W * rng.random((N, 8, L, 16)) ** 4).astype(np.int64), W - 1); o = np.minimum((W * rng.random((N, 8, L, P)) ** 4).astype(np.int64), W - 1)
    d = np.minimum(np.maximum(np.exp2(8 * rng.random((N, 8, 16, L))).astype(np.int64), 1), 255)
    w = rng.integers(0, 16, (N, 8, 16, 1)) * (rng.random((N, 8, 16, 1)) < 0.4)
    return pack(x, c, o, d, w)
def check_inputs(d):
    bad = []
    for k, lo, hi in (("xt", 0, 255), ("pk", 0, W - 1), ("po", 0, W - 1), ("dm", 1, 255), ("wt", 0, 15)):
        v = np.asarray(d[k]).astype(np.float64)
        if not np.all((v >= lo) & (v <= hi) & (v == np.floor(v))): bad.append("range of " + k)
    return bad
def picks(x, z, e, kap):
    return np.take(x, place(z, e, kap) + (W * np.arange(8 * N)).reshape(N, 8, 1, 1), axis=0)
def reference(xt, pk, po, dm, wt):
    x = np.ascontiguousarray(xt.astype(np.float32).astype(np.int32).reshape(8 * N, 16, W).transpose(0, 2, 1)).reshape(-1, 16)
    c = np.stack([gentries(a) for a in pk]).astype(np.int64).reshape(N, 8, L, 16)
    o = np.stack([gentries(a) for a in po]).astype(np.int64).reshape(N, 8, L, P)
    D = np.ascontiguousarray(dm.astype(np.int32).reshape(N, 8, 16, L).transpose(0, 1, 3, 2))
    w = wt.astype(np.int32).reshape(N, 8, 1, 16)
    kap = np.zeros((N, 1, 1, 1), np.int64); left = []
    for t in range(T):
        if t > 0: c = np.roll(c, 1, axis=0)
        e = (np.add.reduce(w * D, axis=3) & 1023).astype(np.int64)
        a = picks(x, c, e, kap); b = picks(x, o, e, kap)
        if t >= N:
            m = left[t - N]; y = picks(x, m, e, kap); gone = (m != c)[..., None]
            up = np.max(np.where(gone, -1, a), axis=3) >= np.max(np.where(gone, y, -1), axis=3)
            D = np.minimum(np.maximum(np.where(up, D + 8, D - 8), 1), 255)
        sa = np.add.reduce(np.minimum(a, D[:, :, :, None, :]), axis=4); sb = np.add.reduce(np.minimum(b, D[:, :, :, None, :]), axis=4)
        k = np.argmax(sa, axis=3)[..., None]; j = np.argmin(sb, axis=3)[..., None]
        swap = np.take_along_axis(sa, k, 3) > np.take_along_axis(sb, j, 3)
        ck = np.take_along_axis(c, k, 3); oj = np.take_along_axis(o, j, 3)
        np.put_along_axis(c, k, np.where(swap, oj, ck), 3); np.put_along_axis(o, j, np.where(swap, ck, oj), 3)
        xk = np.take_along_axis(a, k[..., None], 3)[:, :, :, 0]
        D = np.where(swap & (xk >= D), np.maximum(D - 4, 1), D)
        kap = np.add.reduce(swap.reshape(N, -1).astype(np.int64), axis=1).reshape(N, 1, 1, 1) & 31
        left.append(c)
    return {"yc": np.stack([gtable(v.reshape(8, -1)) for v in c]).astype(np.float32), "yo": np.stack([gtable(v.reshape(8, -1)) for v in o]).astype(np.float32),
            "yd": np.ascontiguousarray(D.transpose(0, 1, 3, 2)).reshape(N, 128, L).astype(np.float32)}

@@ -1,0 +1,531 @@
+from concourse.bass import DstId, RemoteDMATransfer
+from concourse.mybir import dt, AluOpType, AxisListType, ActivationFunctionType
+
+OP = AluOpType
+AF = ActivationFunctionType
+NV = 6
+ZC = 2080
+TW = 2096
+KOFF = 4128.0
+EOFF = 264192.0
+FULL = [(0, 512), (512, 1024)]
+PART = [(0, 512)]
+SHARE = [PART, PART, FULL, PART, FULL, PART]
+
+
+def sb(n, d):
+    return ("sbuf", [128, n], d)
+
+
+F32, B16, F16, I32, U16 = "float32", "bfloat16", "float16", "int32", "uint16"
+SCRATCH = {
+    "pk_i": sb(128, I32), "po_i": sb(256, I32), "dm_i": sb(128, I32), "wt_i": sb(1, I32), "tab": sb(TW, B16),
+    "ic": sb(240, F32), "i8": sb(128, F32), "iperm": sb(128, F32), "ipermf": sb(128, F32), "ienc": sb(128, F32),
+    "ip": sb(1, I32), "pint": sb(4, I32), "pf": sb(4, F32), "pcol": sb(1, F32), "prev": sb(1, F32),
+    "eye16": sb(128, F16), "meye16": sb(128, F16), "r256": sb(256, F16), "perm16": sb(128, F16),
+    "permf16": sb(128, F16), "zb": sb(240, F16), "zfp": sb(240, F16), "zfo": sb(240, F16),
+    "enc16": sb(128, F16), "cpool": sb(256, B16), "onesn": sb(128, B16), "mb": sb(8, F32), "mf": sb(8, F32),
+    "bc": sb(16, U16), "eyeb": sb(128, B16), "m4eye": sb(128, B16), "ones": sb(128, B16),
+    "sel": sb(2048, B16), "wsel": sb(2048, B16), "wcol": sb(1, F32),
+    "pk16": sb(128, F16), "poa16": sb(128, F16), "pob16": sb(128, F16),
+    "q3": sb(384, F16), "rw3": sb(3072, F16), "ya": sb(2048, B16), "yb": sb(2048, B16),
+    "o16": sb(256, F16), "to16": sb(256 * NV, F16),
+    "dt_": sb(128, B16), "dt2": sb(512, B16),
+    "e1": sb(8, B16), "e2": sb(8, F32), "e33": sb(64, F32), "e33w": sb(256, F32),
+    "kf": sb(1, F32), "kr": sb(1, B16), "cnt": sb(1, F32), "cscr": sb(128, F32),
+    "oq": sb(256, I32), "of": sb(256, I32), "ou": sb(256, U16),
+    "pq": sb(128, I32), "pfc": sb(128, I32), "pu": sb(128, U16),
+    "xo": sb(4096, B16), "yo_": sb(4096, B16), "xp": sb(2048, B16), "yp": sb(2080, B16),
+    "losb": sb(64, F32), "w64": sb(64, F32), "w32": sb(32, F32), "w16": sb(16, F32), "m1": sb(8, F32),
+    "sohi": sb(128, F32), "p128": sb(128, F32), "p64": sb(64, F32), "p32": sb(32, F32), "p16": sb(16, F32),
+    "omin": sb(8, F32),
+    "thi": sb(8, I32), "offi": sb(8, I32), "offu": sb(8, U16), "thf": sb(8, F32), "tco": sb(128, F32), "rf": sb(128, F32),
+    "thr": sb(128, F32), "thr2": sb(256, F32), "gt": sb(128, B16),
+    "oh": sb(384, B16), "com": sb(384, F16), "tc16": sb(128, F16),
+    "mq": sb(128, I32), "mfc": sb(128, I32), "mu": sb(128, U16), "mz": sb(128, F32),
+    "stay": sb(128, F32), "sz": sb(128, F32), "au": sb(128, U16),
+    "acc0": sb(512, B16), "acc1": sb(512, B16), "acc2": sb(512, B16), "acc3": sb(512, B16),
+    "ah": sb(256, B16), "bh": sb(256, B16), "amax": sb(128, B16), "bmax": sb(128, B16),
+    "up": sb(128, B16), "up8": sb(128, B16), "dsum": sb(128, F32),
+    "yc_f": sb(128, F32), "yo_f": sb(256, F32), "yd_f": sb(128, F32),
+}
+for _t in range(NV):
+    SCRATCH["c%d" % _t] = sb(128, F16)
+    SCRATCH["n%d" % _t] = sb(128, F16)
+for _b in range(8):
+    SCRATCH["b%d" % _b] = ("psum", [128, 512], F32)
+
+LOADS = ["ld_pk", "ld_po", "ld_dm", "ld_wt", "ld_xt"]
+STORES = ["st_yc", "st_yo", "st_yd"]
+ARR = ["arr%d" % t for t in range(1, NV)]
+SEMAPHORES = ["sv", "sa", "sp", "sg", "loc"] + LOADS + STORES + ARR
+
+CYC, PCYC, CALL, HOP, GATH, WIRE = 0.00091, 0.00079, 0.05, 0.06, 1.5, 4.0
+
+
+EARLY = 4.0
+BOOST = {"cb": -8, "B2.w": 4, "rf": -1, "B2.k": 1, "B7.e": 4, "B5.d": 1, "mu": -2, "up": 1, "B3.o": -1, "B1.s": 2,
+         "obf": -8, "e": -4, "thi": 2, "omin": 4, "thf": -8, "dt": -4, "eye16": -2, "c": 4, "p": 4, "perm16": -2,
+         "offi": -4, "zfo": 2}
+
+
+def rank_program(g, core, T, topo):
+    rank = T.rank_of(core)
+    if rank is None:
+        return
+    nxt = T.cores[(rank + 1) % len(T.cores)]
+    NENG = 8
+    queues = {"V": g.vector, "A": g.scalar, "P": g.tensor, "G": g, "Y": g.sync}
+    counters = {"V": "sv", "A": "sa", "P": "sp", "G": "sg"}
+    v, a_, pe = g.vector, g.scalar, g.tensor
+    boost, boosts = [0.0], []
+    ops = []
+
+    def do(eng, call, reads, writes, dur, lat=0.0, tok=None):
+        ops.append((eng, call, reads, writes, dur, lat, tok))
+        boosts.append(boost[0] + BOOST.get(writes[0].rstrip("012345") if writes else "", 0.0))
+
+    def vec(n):
+        return CALL + max(64, n) * CYC
+
+    def gat(n):
+        return 0.05 + n * GATH * CYC
+
+    def tt(out, x, y, op, r, w, n):
+        do("V", lambda: v.tensor_tensor(out, x, y, op), r, w, vec(n))
+
+    def ttg(out, x, y, op, r, w, n):
+        do("V", lambda: v.tensor_tensor(out, x, y, op), r, w, gat(n))
+
+    def ts(out, x, s1, s2, op0, op1, r, w, n):
+        if op1 is None:
+            do("V", lambda: v.tensor_scalar(out, x, s1, None, op0), r, w, vec(n))
+        else:
+            do("V", lambda: v.tensor_scalar(out, x, s1, s2, op0, op1), r, w, vec(n))
+
+    def cp(out, x, r, w, n):
+        do("V", lambda: v.tensor_copy(out, x), r, w, vec(n))
+
+    def fill(ap, c, w, n):
+        do("V", lambda: v.memset(ap, c), [], w, vec(n))
+
+    def act(out, x, r, w, n, acc=None, scale=1.0, bias=0.0, func=AF.Copy):
+        do("A", lambda: a_.activation(out, x, func, bias=bias, scale=scale, accum_out=acc), r, w, vec(n))
+
+    def actg(out, x, r, w, n):
+        do("A", lambda: a_.activation(out, x, AF.Copy), r, w, gat(n) + 0.015)
+
+    def mm(out, l, x, st, sp, r, w, n):
+        do("P", lambda: pe.matmul(out, l, x, st, sp), r, w, max(64, n) * PCYC)
+
+    def load(eng, sem, out, x, w, lat):
+        do(eng, lambda: queues[eng].dma_start(out, x).then_inc(T.sem[sem], 16), [], [w], 0.1, lat, (sem, 16))
+
+    def store(eng, sem, out, x, r):
+        do(eng, lambda: queues[eng].dma_start(out, x).then_inc(T.sem[sem], 16), r, [], 0.1, 2.0, (sem, 16))
+
+    load("Y", "ld_pk", T.pk_i[:], T.pk[:], "pk_i", 2.0)
+    load("A", "ld_po", T.po_i[:], T.po[:], "po_i", 2.3)
+    load("Y", "ld_dm", T.dm_i[:], T.dm[:], "dm_i", 2.0)
+    load("A", "ld_wt", T.wt_i[:], T.wt[:], "wt_i", 2.0)
+    load("Y", "ld_xt", T.tab[:, 0:2048], T.xt[:], "tab", 3.5)
+
+    def iota(out, pat, base, cm, w, n, small=True):
+        if small:
+            do("G", lambda: g.iota(out, pat, base, cm, allow_small_or_imprecise_dtypes=True), [], w, 0.13 + 2 * n * CYC)
+        else:
+            do("G", lambda: g.iota(out, pat, base, cm), [], w, 0.13 + 2 * n * CYC)
+    iota(T.ip[:], [[0, 1]], 0, 1, ["ip"], 1, False)
+    iota(T.i8[:], [[0, 16], [1, 8]], 0, 0, ["i8"], 128)
+    iota(T.ic[:], [[1, 240]], -112, 0, ["ic"], 240)
+    iota(T.iperm[:], [[16, 8], [-1, 16]], 15, 0, ["iperm"], 128)
+    iota(T.ienc[:], [[128, 16], [16, 8]], 0, 0, ["ienc"], 128)
+    iota(T.cpool[:], [[2, 32], [0, 8]], 0, 0, ["cpool"], 256)
+    iota(T.ipermf[:], [[1, 16], [16, 8]], 0, 0, ["ipermf"], 128)
+    fill(T.wsel[:], 0.0, ["wsel"], 1024)
+    fill(T.kf[:], -KOFF, ["kf"], 1)
+    for j, (op, s) in enumerate([(OP.bitwise_and, 15), (OP.bitwise_and, 7),
+                                 (OP.arith_shift_right, 4), (OP.arith_shift_right, 3)]):
+        ts(T.pint[:, j:j + 1], T.ip[:], s, None, op, None, ["ip"], ["pint%d" % j], 1)
+    cp(T.pcol[:], T.ip[:], ["ip"], ["pcol"], 1)
+    cp(T.pf[:], T.pint[:], ["pint%d" % j for j in range(4)], ["pf"], 4)
+    ic0 = T.ic[:, 112:240]
+    P16, P8, D16, D8 = (T.pf[:, j:j + 1] for j in range(4))
+    PC, EQ = T.pcol[:], OP.is_equal
+    ts(T.mb[:], T.i8[:, 0:8], D16, None, EQ, None, ["i8", "pf"], ["mb"], 8)
+    ts(T.zb[:], T.ic[:], P16, None, EQ, None, ["ic", "pf"], ["zb"], 240)
+    act(T.ones[:], T.ic[:, 0:128], ["ic"], ["ones"], 128, None, 0.0, 1.0)
+    do("G", lambda: g.affine_select(T.eyeb[:], T.ones[:], [[-1, 128]], EQ, 0.0, 0, 1), ["ones"], ["eyeb"], 0.4)
+    ts(T.eye16[:], ic0, PC, None, EQ, None, ["ic", "pcol"], ["eye16"], 128)
+    ts(T.bc[:], T.i8[:, 0:16], 0.0, P8, OP.mult, OP.add, ["i8", "pf"], ["bc"], 16)
+    ts(T.perm16[:], T.iperm[:], PC, None, EQ, None, ["iperm", "pcol"], ["perm16"], 128)
+    selz = ["selz%d" % i for i in range(0, 2048, 240)]
+    for i in range(0, 2048, 240):
+        n = min(240, 2048 - i)
+        act(T.sel[:, i:i + n], T.ic[:, 0:n], ["ic"], ["selz%d" % i], n, None, 0.0)
+    act(T.tab[:, 2080:TW], T.ic[:, 0:16], ["ic"], ["tabz"], 16, None, 0.0)
+    act(T.yp[:, 2048:2080], T.ic[:, 0:32], ["ic"], ["ypz"], 32, None, 0.0)
+    act(T.onesn[:], T.ic[:, 0:128], ["ic"], ["onesn"], 128, None, 0.0, 0.0078125)
+    act(T.cpool[0:64, 0:240], T.ic[0:64, :], ["ic"], ["cpool"], 240, None, 0.0, 4096.0)
+    act(T.cpool[0:64, 240:256], T.ic[0:64, 0:16], ["ic"], ["cpool"], 16, None, 0.0, 4096.0)
+    act(T.m4eye[:], T.eyeb[:], ["eyeb"], ["m4eye"], 128, None, -4.0)
+    ts(T.sel[:, 0:2048:16], T.i8[:], D16, 4096.0, EQ, OP.mult, ["i8", "pf"] + selz, ["sel"], 128)
+    ts(T.enc16[:], T.ienc[:], P16, None, OP.add, None, ["ienc", "pf"], ["enc16"], 128)
+    ts(T.meye16[:], T.eye16[:], -1.0, None, OP.mult, None, ["eye16"], ["meye16"], 64)
+    ts(T.rf[:], T.i8[:], P8, None, EQ, None, ["i8", "pf"], ["rf"], 128)
+    for j in range(2):
+        ts(T.r256[:, 128 * j:128 * j + 128], T.rf[:], -1.0, None, OP.mult, None, ["rf"], ["r256"], 128)
+    boost[0] = EARLY
+    cp(T.dt_[:], T.dm_i[:], ["dm_i"], ["dt"], 128)
+    ts(T.wcol[:], T.wt_i[:], 2.0, None, OP.mult, None, ["wt_i"], ["wcol"], 1)
+    ts(T.wsel[:, 0:2048:16], T.i8[:], D16, T.wcol[:], EQ, OP.mult, ["i8", "pf", "wcol", "wsel"], ["wsel"], 128)
+    boost[0] = 0.0
+    act(T.tab[:, 2048:2080], T.tab[:, 0:32], ["tab"], ["tabx"], 32)
+    tabk = ["tab", "tabx", "tabz"]
+    win = T.tab[:, 0:TW]
+
+    def seats_e():
+        for a in range(16):
+            mm(T.b7[:, 128:136], T.wsel[:, 127 * a:127 * a + 128], T.dt_[:, a:128:16], a == 0, a == 15,
+               ["wsel", "dt"], ["B7.e"], 8)
+        act(T.e1[:], T.b7[:, 128:136], ["B7.e"], ["e1"], 8, None, 1.0, EOFF - 1023.0)
+        tt(T.e2[:], T.b7[:, 128:136], T.e1[:], OP.subtract, ["B7.e", "e1"], ["e2"], 8)
+        do("V", lambda: v.tensor_scalar(T.e33[:], T.e2[:].indirect(T.bc[:, 0:4]), 1.0, EOFF + 33.0, OP.mult, OP.add),
+           ["e2", "bc"], ["e33"], gat(64))
+        for i in range(4):
+            act(T.e33w[:, 64 * i:64 * i + 64], T.e33[:], ["e33"], ["e33w%d" % i], 64)
+
+    def spread_d(fused=True):
+        for i in range(4):
+            mm(T.b5[:, 128 * i:128 * i + 128], T.eyeb[:], T.dt_[:], True, True, ["eyeb", "dt"], ["B5.d"], 128)
+        if fused:
+            act(T.dt2[:], T.b5[:], ["B5.d", "e33"], ["dt2"], 512)
+
+    def index(cards, ck, qb, fb, n0, n1, outs, nm):
+        s, n = slice(n0, n1), n1 - n0
+        ek = ["e33w%d" % i for i in range((n + 63) // 64)]
+        cyc = n if ck[0] == "B" else 2 * n
+        if n == 64:
+            tt(qb[:, s], cards, T.e33[:], OP.mult, [ck, "e33"], [nm + "q"], cyc)
+        else:
+            tt(qb[:, s], cards, T.e33w[:, 0:n], OP.mult, [ck] + ek, [nm + "q"], cyc)
+        ts(fb[:, s], qb[:, s], 5, 2047, OP.arith_shift_right, OP.bitwise_and, [nm + "q"], [nm + "f"], n)
+        for out, z, key in outs:
+            ts(out[:, s], fb[:, s], T.kf[:], KOFF + z, OP.add, OP.add, [nm + "f", "kf"], [key], n)
+
+    def block(x, y, off, base, pieces, nm, uk):
+        keys = []
+        end = base + pieces[-1][1]
+        for lo, hi in pieces:
+            lo, hi = lo + base, hi + base
+            actg(x[:, lo:hi], win.indirect(off[:, lo // 16:hi // 16]), tabk + [uk], [nm + "x%d" % lo], hi - lo)
+        if end < base + 1024:
+            ttg(y[:, end:base + 1024], win.indirect(off[:, end // 16:(base + 1024) // 16]),
+                T.dt2[:, 0:base + 1024 - end], OP.min, tabk + [uk, "dt2"], [nm + "f%d" % end], base + 1024 - end)
+            keys.append(nm + "f%d" % end)
+        for lo, hi in pieces:
+            lo, hi = lo + base, hi + base
+            tt(y[:, lo:hi], x[:, lo:hi], T.b5[:, 0:hi - lo], OP.min, [nm + "x%d" % lo, "B5.d"], [nm + "y%d" % lo], hi - lo)
+            keys.append(nm + "y%d" % lo)
+        return keys
+
+    def scores(out, k, const, l, ck, y, base, keys):
+        mm(out, l, const, True, False, ck, [k], 64)
+        for a in range(16):
+            mm(out, T.sel[:, 127 * a:127 * a + 128], y[:, base + a:base + 1024:16], False, a == 15, ["sel"] + keys, [k], 64)
+
+    def pools(t, share):
+        index(T.b3[:, 0:64], "B3.o", T.oq, T.of, 0, 64, [(T.ou, 0.0, "oua")], "oa")
+        index(T.b3[:, 64:256], "B3.o", T.oq, T.of, 64, 256, [(T.ou, 0.0, "oub")], "ob")
+        for c in range(4):
+            keys = block(T.xo, T.yo_, T.ou, 1024 * c, share[c], "o", "oub" if c else "oua")
+            scores(T.b0[:, 64 * c:64 * c + 64], "B0.s", T.cpool[:, 64 * c:64 * c + 64], T.onesn[:], ["onesn", "cpool"],
+                   T.yo_, 1024 * c, keys)
+
+    def pool_min():
+        act(T.sohi[:], T.b0[:, 128:256], ["B0.s"], ["sohi"], 128)
+        tt(T.p128[:], T.b0[:, 0:128], T.sohi[:], OP.min, ["B0.s", "sohi"], ["p128"], 128)
+        tt(T.p64[:], T.p128[:, 0:64], T.p128[:, 64:128], OP.min, ["p128"], ["p64"], 128)
+        tt(T.p32[:], T.p64[:, 0:32], T.p64[:, 32:64], OP.min, ["p64"], ["p32"], 64)
+        tt(T.p16[:], T.p32[:, 0:16], T.p32[:, 16:32], OP.min, ["p32"], ["p16"], 32)
+        tt(T.omin[:], T.p16[:, 0:8], T.p16[:, 8:16], OP.min, ["p16"], ["omin"], 16)
+
+    def pool_card(t):
+        actg(T.thr2[:], T.omin[:].indirect(T.bc[:]), ["omin", "bc"], ["thr2"], 256)
+        tt(T.oh[:, 128:384], T.b0[:, 0:256], T.thr2[:], EQ, ["B0.s", "thr2"], ["oho"], 256)
+        tt(T.com[:, 128:384], T.oh[:, 128:384], T.b3[:, 0:256], OP.mult, ["oho", "B3.o"], ["com"], 256)
+        mm(T.b3[:, 0:256], T.eye16[:], T.o16[:], True, False, ["eye16", "o16"], ["B3.o"], 256)
+        for u in range(t):
+            mm(T.b3[:, 0:256], T.eye16[:], T.to16[:, 256 * u:256 * u + 256], False, False, ["eye16", "to%d" % u],
+               ["B3.o"], 256)
+        for j in range(2):
+            mm(T.b6[:, 0:128], T.com[:, 128 + 128 * j:256 + 128 * j], T.eye16[:], j == 0, j == 1, ["com", "eye16"],
+               ["B6.t0"], 128)
+        act(T.tco[:], T.b6[:, 0:128], ["B6.t0"], ["tco"], 128)
+        mm(T.b2[:, 128:256], T.tco[:], T.rf[:], True, False, ["tco", "rf"], ["B2.w"], 512)
+        mm(T.b2[:, 128:256], T.meye16[:], T["c%d" % t][:], False, True, ["meye16", "c%d" % t], ["B2.w"], 128)
+
+    def pack_index(t):
+        boost[0] = 5.0
+        index(T.b4[:, 0:128], "B4.c", T.pq, T.pfc, 0, 128, [(T.pu, 0.0, "pu")], "p")
+        boost[0] = 0.0
+
+    def packs(t, share):
+        all_keys = []
+        for c in range(2):
+            keys = block(T.xp, T.yp, T.pu, 1024 * c, share[4 + c], "p", "pu")
+            scores(T.b1[:, 64 * c:64 * c + 64], "B1.s%d" % c, T.enc16[:, 64 * c:64 * c + 64], T.eye16[:],
+                   ["eye16", "enc16"], T.yp, 1024 * c, keys)
+            all_keys += keys
+            if c == 0:
+                act(T.losb[:], T.b1[:, 0:64], ["B1.s0"], ["losb"], 64)
+        tt(T.w64[:], T.b1[:, 64:128], T.losb[:], OP.max, ["B1.s1", "losb"], ["w64"], 64)
+        tt(T.w32[:], T.w64[:, 0:32], T.w64[:, 32:64], OP.max, ["w64"], ["w32"], 64)
+        tt(T.w16[:], T.w32[:, 0:16], T.w32[:, 16:32], OP.max, ["w32"], ["w16"], 32)
+        tt(T.m1[:], T.w16[:, 0:8], T.w16[:, 8:16], OP.max, ["w16"], ["m1"], 16)
+        return all_keys
+
+    def pack_to_psum(t):
+        mm(T.b4[:, 0:128], T.eye16[:], T["c%d" % t][:], True, True, ["eye16", "c%d" % t], ["B4.c"], 128)
+
+    def send(t):
+        rid, pid, _ = topo.addr(nxt)
+        m = 0
+        for en in topo.engines(core, nxt)[:NENG]:
+            m |= 1 << en
+        sem = "arr%d" % (t + 1)
+        src, dst = T["n%d" % t][:], T["c%d" % (t + 1)][:]
+        do("G", lambda: g.remote_dma(dst, src, T.sem[sem], T.sem.loc, pid, rid, m), ["n%d" % t], ["c%d" % (t + 1)],
+           1.0, WIRE, (sem, NENG))
+
+    def exchange(t, ykeys):
+        last = t == NV - 1
+        mo = ["m1", "omin"]
+        tt(T.thi[:], T.m1[:], T.omin[:], OP.max, mo, ["thi"], 16)
+        tt(T.thf[:], T.m1[:], T.omin[:], OP.max, mo, ["thf"], 16)
+        ts(T.offi[:], T.thi[:], 4095, None, OP.bitwise_and, None, ["thi"], ["offi"], 8)
+        cp(T.offu[:], T.offi[:], ["offi"], ["offu"], 8)
+        actg(T.thr[:], T.thf[:].indirect(T.bc[:, 0:8]), ["thf", "bc"], ["thr"], 128)
+        ttg(T.gt[:], T.yp[:].indirect(T.offu[:]), T.dt_[:], OP.is_ge, ykeys + ["ypz", "offu", "dt"], ["gt"], 128)
+        mm(T.b7[:, 0:128], T.eyeb[:], T.dt_[:], True, False, ["eyeb", "dt"], ["B7.d"], 128)
+        mm(T.b7[:, 0:128], T.m4eye[:], T.gt[:], False, True, ["m4eye", "gt"], ["B7.d"], 128)
+        ts(T.dt_[:], T.b7[:, 0:128], 1.0, None, OP.max, None, ["B7.d"], ["dt"], 128)
+        if last:
+            act(T.yd_f[:], T.dt_[:], ["dt"], ["yd_f"], 128)
+            store("Y", "st_yd", T.yd[:], T.yd_f[:], ["yd_f"])
+        tt(T.oh[:, 0:128], T.b1[:, 0:128], T.thr[:], OP.is_ge, ["B1.s0", "B1.s1", "thr"], ["ohc"], 128)
+        tt(T.com[:, 0:128], T.oh[:, 0:128], T.b2[:, 128:256], OP.mult, ["ohc", "B2.w"], ["tuc"], 128)
+        tt(T["n%d" % t][:], T.com[:, 0:128], T.b4[:, 0:128], OP.add, ["tuc", "B4.c"], ["n%d" % t], 128)
+        if not last:
+            send(t)
+        mm(T.b6[:, 128:256], T.com[:, 0:128], T.eye16[:], True, True, ["tuc", "eye16"], ["B6.t"], 128)
+        if not last:
+            mm(T.b2[:, 0:128], T.ones[:], T.oh[:, 0:128], True, True, ["ones", "ohc"], ["B2.k"], 128)
+            act(T.cscr[:], T.b2[:, 0:128], ["B2.k"], ["cnt", "cscr"], 128, T.cnt[:])
+            act(T.kr[:], T.cnt[:], ["cnt"], ["kr"], 1, None, 1.0, KOFF - 15.5)
+            do("A", lambda: a_.activation(T.kf[:], T.kr[:], AF.Identity, bias=T.cnt[:], scale=-1.0), ["kr", "cnt"],
+               ["kf"], vec(1))
+            seats_e()
+        cp(T.tc16[:], T.b6[:, 128:256], ["B6.t"], ["tc16"], 128)
+        mm(T.b6[:, 256:512], T.tc16[:], T.r256[:], True, True, ["tc16", "r256"], ["B6.d"], 256)
+        to = T.to16[:, 256 * t:256 * t + 256]
+        tt(to, T.oh[:, 128:384], T.b6[:, 256:512], OP.mult, ["oho", "B6.d"], ["to%d" % t], 256)
+        mm(T.b3[:, 0:256], T.eye16[:], to, False, True, ["eye16", "to%d" % t], ["B3.o"], 256)
+        if not last:
+            spread_d(t < NV - 2)
+
+    Q = [T.q3[:, 128 * i:128 * i + 128] for i in range(3)]
+    RW = [T.rw3[:, 1024 * i:1024 * i + 1024] for i in range(3)]
+    BK = [T.b0, T.b1, T.b2]
+    cp(T.pk16[:], T.pk_i[:], ["pk_i"], ["pk16"], 128)
+    cp(T.poa16[:], T.po_i[:, 0:256:2], ["po_i"], ["poa16"], 128)
+    cp(T.pob16[:], T.po_i[:, 1:256:2], ["po_i"], ["pob16"], 128)
+    boost[0] = EARLY
+    seats_e()
+    boost[0] = 0.0
+    for i, (src, p) in enumerate([("pk16", "perm16"), ("poa16", "eye16"), ("pob16", "eye16")]):
+        mm(T.b0[:, 128 * i:128 * i + 128], T[src][:], T[p][:], True, True, [src, p], ["B0.q%d" % i], 128)
+    cp(T.q3[:], T.b0[:, 0:384], ["B0.q0", "B0.q1", "B0.q2"], ["q3"], 384)
+    for b in range(8):
+        ts(T.rw3[:, b:3072:8], T.q3[:], T.mb[:, b:b + 1], None, OP.mult, None, ["q3", "mb"], ["rw%d" % b], 192)
+    for i, (out, k) in enumerate([(T.b4[:, 0:128], "B4.c"), (T.b3[:, 0:128], "B3.o"), (T.b3[:, 128:256], "B3.o")]):
+        for x in range(8):
+            mm(out, T.zb[:, 112 - 16 * x:240 - 16 * x], T.rw3[:, 1024 * i + 128 * x:1024 * i + 128 * x + 128],
+               x == 0, x == 7, ["zb"] + ["rw%d" % b for b in range(8)], [k], 128)
+    cp(T.c0[:], T.b4[:, 0:128], ["B4.c"], ["c0"], 128)
+    spread_d()
+    pack_index(0)
+    cp(T.o16[:], T.b3[:, 0:256], ["B3.o"], ["o16"], 256)
+
+    for t in range(NV - 1):
+        share = SHARE
+        pools(t, share)
+        pool_min()
+        pool_card(t)
+        if t:
+            pack_to_psum(t)
+            pack_index(t)
+        exchange(t, packs(t, share))
+
+    t = NV - 1
+
+    def chain(off, okey, y, acc, half, out, key):
+        two = key == "cb"
+        for i in range(2 if two else 3):
+            actg(y[:, 512 * i:512 * i + 512], win.indirect(off[:, 32 * i:32 * i + 32]), tabk + [okey], [key + "g%d" % i], 512)
+        ttg(acc[0][:], win.indirect(off[:, 96:128]), y[:, 0:512], OP.max, tabk + [okey, key + "g0"], [key + "0"], 512)
+        if two:
+            ttg(acc[1][:], win.indirect(off[:, 64:96]), acc[0][:], OP.max, tabk + [okey, key + "0"], [key + "1"], 512)
+        for i, b in ((2, T.b6),) if two else ((1, T.b2), (2, T.b6)):
+            bk = ("B2." if i == 1 else "B6.") + key
+            q = i - 1 if two else i
+            mm(b[:], T.eyeb[:], y[:, 512 * q:512 * q + 512], True, True, ["eyeb", key + "g%d" % q], [bk], 512)
+            if i == 1:
+                tt(acc[1][:], acc[0][:], b[:], OP.max, [key + "0", bk], [key + "1"], 512)
+            else:
+                tt(acc[0][:, 0:256], acc[1][:, 0:256], b[:, 0:256], OP.max, [key + "1", bk], [key + "2"], 256)
+                tt(T.b0[:, 0:256], acc[1][:, 256:512], b[:, 256:512], OP.max, [key + "1", bk], ["B0." + key], 256)
+        tt(half[:], acc[0][:, 0:256], T.b0[:, 0:256], OP.max, [key + "2", "B0." + key], [key + "h"], 256)
+        tt(out[0], half[:, 0:128], half[:, 128:256], OP.max, [key + "h"], [out[1]], 256)
+    index(T.n0[:], "n0", T.mq, T.mfc, 0, 128, [(T.mu, 0.0, "mu"), (T.mz, -float(ZC), "mz")], "m")
+    chain(T.mu, "mu", T.yb, [T.acc0, T.acc1], T.bh, (T.b1[:, 0:128], "B1.bm"), "cb")
+    pack_to_psum(t)
+    pack_index(t)
+    tt(T.b4[:, 128:256], T.n0[:], T.b4[:, 0:128], EQ, ["n0", "B4.c"], ["B4.stay"], 128)
+    tt(T.sz[:], T.b4[:, 128:256], T.mz[:], OP.mult, ["B4.stay", "mz"], ["sz"], 128)
+    ts(T.au[:], T.sz[:], float(ZC), None, OP.add, None, ["sz"], ["au"], 128)
+    chain(T.au, "au", T.ya, [T.acc2, T.acc3], T.ah, (T.amax[:], "cam"), "ca")
+    tt(T.up[:], T.amax[:], T.b1[:, 0:128], OP.is_ge, ["cam", "B1.bm"], ["up"], 128)
+    ts(T.b4[:, 384:512], T.up[:], 16.0, -8.0, OP.mult, OP.add, ["up"], ["B4.up8"], 128)
+    tt(T.dsum[:], T.dt_[:], T.b4[:, 384:512], OP.add, ["dt", "B4.up8"], ["dsum"], 128)
+    ts(T.dt_[:], T.dsum[:], 1.0, 255.0, OP.max, OP.min, ["dsum"], ["dt"], 128)
+    spread_d(False)
+    pools(t, [FULL] * 6)
+    pool_min()
+    pool_card(t)
+    exchange(t, packs(t, [FULL] * 6))
+
+    ts(T.permf16[:], T.ipermf[:], PC, None, EQ, None, ["ipermf", "pcol"], ["permf16"], 128)
+    ts(T.prev[:], D8, -1.0, 15.0, OP.mult, OP.add, ["pf"], ["prev"], 1)
+    ts(T.mf[:], T.i8[:, 0:8], P8, None, EQ, None, ["i8", "pf"], ["mf"], 8)
+    ts(T.zfo[:], T.ic[:], D8, None, EQ, None, ["ic", "pf"], ["zfo"], 240)
+    ts(T.zfp[:], T.ic[:], T.prev[:], None, EQ, None, ["ic", "prev"], ["zfp"], 240)
+
+    def seats_to_list(i, src, skey, z, zk, out, ok, dst, dk):
+        k = "B%d.f" % i
+        mm(BK[i][:, 384:512], src, T.permf16[:], True, True, [skey, "permf16"], [k], 128)
+        cp(Q[i], BK[i][:, 384:512], [k], ["q%d" % i], 128)
+        for b in range(8):
+            ts(RW[i][:, 128 * b:128 * b + 128], Q[i], T.mf[:, b:b + 1], None, OP.mult, None, ["q%d" % i, "mf"],
+               ["rx%d%d" % (i, b)], 64)
+        for x in range(8):
+            mm(out, z[:, 112 - 16 * x:240 - 16 * x], RW[i][:, x:1024:8], x == 0, x == 7,
+               [zk] + ["rx%d%d" % (i, b) for b in range(8)], [ok], 128)
+        act(dst, out, [ok], [dk], 128)
+    oe, oek = T.o16[:], "o16"
+    cp(oe, T.b3[:, 0:256], ["B3.o"], [oek], 256)
+    seats_to_list(0, T["n%d" % t][:], "n%d" % t, T.zfp, "zfp", T.b4[:, 0:128], "B4.y", T.yc_f[:], "yc_f")
+    seats_to_list(1, oe[:, 0:128], oek, T.zfo, "zfo", T.b5[:, 0:128], "B5.y", T.yo_f[:, 0:256:2], "yo_f0")
+    seats_to_list(2, oe[:, 128:256], oek, T.zfo, "zfo", T.b7[:, 0:128], "B7.y", T.yo_f[:, 1:256:2], "yo_f1")
+    store("Y", "st_yc", T.yc[:], T.yc_f[:], ["yc_f"])
+    store("Y", "st_yo", T.yo[:], T.yo_f[:], ["yo_f0", "yo_f1"])
+
+    n = len(ops)
+    preds = [{} for _ in range(n)]
+    lastw, readers, bankacc = {}, {}, {}
+    for i, (eng, call, reads, writes, dur, lat, tok) in enumerate(ops):
+        def edge(j, wait, i=i):
+            if j != i:
+                preds[i][j] = preds[i].get(j, False) or wait
+        for k in reads:
+            if k in lastw:
+                edge(lastw[k], True)
+        for k in writes:
+            if k in lastw:
+                edge(lastw[k], ops[lastw[k]][0] != eng)
+            for j in readers.get(k, []):
+                edge(j, ops[j][0] != eng or ops[j][6] is not None)
+        for k in sorted({k[:2] for k in reads + writes if k[0] == "B"}):
+            turn = bankacc.setdefault(k, [eng, [], []])
+            if turn[0] != eng:
+                turn[0], turn[1], turn[2] = eng, turn[2], []
+            for j in turn[1]:
+                edge(j, True)
+            if eng == "P" and turn[2]:
+                edge(turn[2][-1], False)
+            turn[2].append(i)
+        for k in reads:
+            readers.setdefault(k, []).append(i)
+        for k in writes:
+            lastw[k] = i
+            readers[k] = []
+    succs = [[] for _ in range(n)]
+    for i in range(n):
+        for j in preds[i]:
+            succs[j].append(i)
+    prio = [0.0] * n
+    for i in range(n - 1, -1, -1):
+        own = ops[i][4] + ops[i][5]
+        best = 0.0
+        for s in succs[i]:
+            best = max(best, prio[s] + (own + HOP if preds[s][i] else ops[i][4]))
+        prio[i] = max(best, own)
+
+    left = [len(p) for p in preds]
+    est = [0.0] * n
+    ready = {e: [] for e in queues}
+    free = {e: 0.0 for e in queues}
+    for i in range(n):
+        if left[i] == 0:
+            ready[ops[i][0]].append(i)
+    sequence = []
+    for _ in range(n):
+        pick = None
+        for e in queues:
+            if ready[e]:
+                st = max(free[e], min(est[i] for i in ready[e]))
+                i = max((i for i in ready[e] if est[i] <= st + 1e-9), key=lambda i: (prio[i] + boosts[i], -i))
+                if pick is None or st < pick[0]:
+                    pick = (st, e, i)
+        st, e, i = pick
+        ready[e].remove(i)
+        sequence.append(i)
+        free[e] = st + ops[i][4]
+        for s in succs[i]:
+            est[s] = max(est[s], free[e] + (ops[i][5] + HOP if preds[s][i] else 0.0))
+            left[s] -= 1
+            if left[s] == 0:
+                ready[ops[s][0]].append(s)
+
+    count = {e: 0 for e in counters}
+    waited = {e: {} for e in queues}
+    token = {}
+
+    def need(e, tok):
+        s, c = tok
+        if waited[e].get(s, 0) < c:
+            queues[e].wait_ge(T.sem[s], c)
+            waited[e][s] = c
+
+    for i in sequence:
+        eng, call, reads, writes, dur, lat, tok = ops[i]
+        toks = {}
+        for j, w in preds[i].items():
+            if w and token[j][1] > toks.get(token[j][0], 0):
+                toks[token[j][0]] = token[j][1]
+        for s in toks:
+            need(eng, (s, toks[s]))
+        if tok is None:
+            count[eng] += 1
+            call().then_inc(T.sem[counters[eng]], 1)
+            token[i] = (counters[eng], count[eng])
+        else:
+            call()
+            token[i] = tok
+    for e in counters:
+        need("G", (counters[e], count[e]))
+    for s in LOADS + STORES:
+        need("G", (s, 16))
+    need("G", ("loc", NENG * len(ARR)))
+    for s in ARR:
+        need("G", (s, NENG))

@@ -4,13 +4,16 @@ from concourse.mybir import dt, AluOpType, AxisListType, ActivationFunctionType
 OP = AluOpType
 AF = ActivationFunctionType
 NV = 6
-ZC = 2080
-TW = 2096
+W = 2048
+TW = 2080
 KOFF = 4128.0
-EOFF = 264192.0
-FULL = [(0, 512), (512, 1024)]
-PART = [(0, 512)]
-SHARE = [PART, PART, FULL, PART, FULL, PART]
+BIG = 67108864.0
+LV = 72
+VCH = [(0, 32), (32, 64), (64, LV)]
+VCALL = [[(0, 32), (32, LV)], [(0, LV)], [(0, LV)]]
+ACH = [(LV, 100), (100, 128)]
+LV5 = 64
+V5RAW = 2
 
 
 def sb(n, d):
@@ -19,34 +22,28 @@ def sb(n, d):
 
 F32, B16, F16, I32, U16 = "float32", "bfloat16", "float16", "int32", "uint16"
 SCRATCH = {
-    "pk_i": sb(128, I32), "po_i": sb(256, I32), "dm_i": sb(128, I32), "wt_i": sb(1, I32), "tab": sb(TW, B16),
-    "ic": sb(240, F32), "i8": sb(128, F32), "iperm": sb(128, F32), "ipermf": sb(128, F32), "ienc": sb(128, F32),
-    "ip": sb(1, I32), "pint": sb(4, I32), "pf": sb(4, F32), "pcol": sb(1, F32), "prev": sb(1, F32),
-    "eye16": sb(128, F16), "meye16": sb(128, F16), "r256": sb(256, F16), "perm16": sb(128, F16),
-    "permf16": sb(128, F16), "zb": sb(240, F16), "zfp": sb(240, F16), "zfo": sb(240, F16),
-    "enc16": sb(128, F16), "cpool": sb(256, B16), "onesn": sb(128, B16), "mb": sb(8, F32), "mf": sb(8, F32),
-    "bc": sb(16, U16), "eyeb": sb(128, B16), "m4eye": sb(128, B16), "ones": sb(128, B16),
-    "sel": sb(2048, B16), "wsel": sb(2048, B16), "wcol": sb(1, F32),
-    "pk16": sb(128, F16), "poa16": sb(128, F16), "pob16": sb(128, F16),
-    "q3": sb(384, F16), "rw3": sb(3072, F16), "ya": sb(2048, B16), "yb": sb(2048, B16),
+    "pk_i": sb(128, I32), "po_i": sb(256, I32), "dm_i": sb(128, I32), "wt_i": sb(1, I32),
+    "tab": sb(TW, B16), "ntab": sb(TW, B16), "tab5": sb(2 * TW, F32),
+    "ip": sb(1, I32), "pint": sb(2, I32), "pf": sb(2, F32), "icol": sb(128, F32), "idiv": sb(128, F32),
+    "imod": sb(128, F32), "i16q": sb(128, F32), "icp": sb(128, F32), "ico": sb(256, F32), "ijt": sb(256, F32),
+    "fours": sb(W, B16), "rep4": sb(W, B16), "ones": sb(128, B16), "eyeb": sb(128, B16), "neye": sb(128, B16),
+    "eye5": sb(128, B16), "n4eye": sb(128, B16), "eye16": sb(256, F16), "neye16": sb(128, F16),
+    "bo16": sb(128, F16), "nbo16": sb(128, F16), "g4": sb(8, B16), "rb16": sb(8, F16), "bc8": sb(8, U16),
+    "mask": sb(128, F32), "enc": sb(128, F32), "jt": sb(256, F32), "cp16": sb(128, F16), "co16": sb(256, F16),
+    "rsp": sb(128, F32), "rso": sb(256, F32), "ec": sb(128, B16),
+    "wcol": sb(1, F32), "w2b": sb(128, B16), "w10b": sb(128, B16), "nw2b": sb(128, B16), "w2h": sb(128, F16),
     "o16": sb(256, F16), "to16": sb(256 * NV, F16),
-    "dt_": sb(128, B16), "dt2": sb(512, B16),
-    "e1": sb(8, B16), "e2": sb(8, F32), "e33": sb(64, F32), "e33w": sb(256, F32),
-    "kf": sb(1, F32), "kr": sb(1, B16), "cnt": sb(1, F32), "cscr": sb(128, F32),
-    "oq": sb(256, I32), "of": sb(256, I32), "ou": sb(256, U16),
-    "pq": sb(128, I32), "pfc": sb(128, I32), "pu": sb(128, U16),
-    "xo": sb(4096, B16), "yo_": sb(4096, B16), "xp": sb(2048, B16), "yp": sb(2080, B16),
-    "losb": sb(64, F32), "w64": sb(64, F32), "w32": sb(32, F32), "w16": sb(16, F32), "m1": sb(8, F32),
-    "sohi": sb(128, F32), "p128": sb(128, F32), "p64": sb(64, F32), "p32": sb(32, F32), "p16": sb(16, F32),
-    "omin": sb(8, F32),
-    "thi": sb(8, I32), "offi": sb(8, I32), "offu": sb(8, U16), "thf": sb(8, F32), "tco": sb(128, F32), "rf": sb(128, F32),
-    "thr": sb(128, F32), "thr2": sb(256, F32), "gt": sb(128, B16),
-    "oh": sb(384, B16), "com": sb(384, F16), "tc16": sb(128, F16),
-    "mq": sb(128, I32), "mfc": sb(128, I32), "mu": sb(128, U16), "mz": sb(128, F32),
-    "stay": sb(128, F32), "sz": sb(128, F32), "au": sb(128, U16),
-    "acc0": sb(512, B16), "acc1": sb(512, B16), "acc2": sb(512, B16), "acc3": sb(512, B16),
-    "ah": sb(256, B16), "bh": sb(256, B16), "amax": sb(128, B16), "bmax": sb(128, B16),
-    "up": sb(128, B16), "up8": sb(128, B16), "dsum": sb(128, F32),
+    "d": sb(128, B16), "dtr": sb(128, B16), "ndtr": sb(128, B16), "dec": sb(128, B16), "z": sb(128, F32),
+    "dsp": sb(16 * LV, B16), "e1": sb(128, B16), "e33": sb(128, F32),
+    "kacc": sb(1, F32), "kr": sb(1, B16), "kf": sb(1, F32), "kscr": sb(128, F32),
+    "iq": sb(512, I32), "jf": sb(512, I32), "iu": sb(384, U16), "mz": sb(128, F32), "mt": sb(128, F32),
+    "au": sb(128, U16),
+    "xr": sb(3 * W, B16), "yo_": sb(2 * W, B16), "yp": sb(W + 48, B16),
+    "so": sb(256, F32), "sp_": sb(128, F32), "omax": sb(8, I32), "ol": sb(8, I32), "thi": sb(8, I32),
+    "tl": sb(8, I32), "uo": sb(128, F16), "up": sb(128, F16), "mk": sb(128, F16), "offu": sb(8, U16),
+    "oho": sb(256, B16), "como": sb(256, F16), "ohp": sb(128, B16), "comp": sb(128, F16), "keep": sb(128, F16),
+    "v5": sb(W, F32), "s5": sb(W, F32), "vi": sb(128, I32), "vu": sb(128, I32), "dlo": sb(128, B16),
+    "dhi": sb(128, B16), "ud": sb(128, B16),
     "yc_f": sb(128, F32), "yo_f": sb(256, F32), "yd_f": sb(128, F32),
 }
 for _t in range(NV):
@@ -55,18 +52,13 @@ for _t in range(NV):
 for _b in range(8):
     SCRATCH["b%d" % _b] = ("psum", [128, 512], F32)
 
-LOADS = ["ld_pk", "ld_po", "ld_dm", "ld_wt", "ld_xt"]
+LOADS = ["ld_dm", "ld_wt", "ld_po", "ld_x0", "ld_x1", "ld_pk"]
 STORES = ["st_yc", "st_yo", "st_yd"]
 ARR = ["arr%d" % t for t in range(1, NV)]
 SEMAPHORES = ["sv", "sa", "sp", "sg", "loc"] + LOADS + STORES + ARR
 
-CYC, PCYC, CALL, HOP, GATH, WIRE = 0.00091, 0.00079, 0.05, 0.06, 1.5, 4.0
-
-
-EARLY = 4.0
-BOOST = {"cb": -8, "B2.w": 4, "rf": -1, "B2.k": 1, "B7.e": 4, "B5.d": 1, "mu": -2, "up": 1, "B3.o": -1, "B1.s": 2,
-         "obf": -8, "e": -4, "thi": 2, "omin": 4, "thf": -8, "dt": -4, "eye16": -2, "c": 4, "p": 4, "perm16": -2,
-         "offi": -4, "zfo": 2}
+CYC, PCYC, CALL, HOP, GATH, WIRE = 0.00091, 0.0007, 0.05, 0.06, 1.5, 3.5
+BOOST = {"tab5": -30.0}
 
 
 def rank_program(g, core, T, topo):
@@ -78,215 +70,220 @@ def rank_program(g, core, T, topo):
     queues = {"V": g.vector, "A": g.scalar, "P": g.tensor, "G": g, "Y": g.sync}
     counters = {"V": "sv", "A": "sa", "P": "sp", "G": "sg"}
     v, a_, pe = g.vector, g.scalar, g.tensor
-    boost, boosts = [0.0], []
     ops = []
 
-    def do(eng, call, reads, writes, dur, lat=0.0, tok=None):
-        ops.append((eng, call, reads, writes, dur, lat, tok))
-        boosts.append(boost[0] + BOOST.get(writes[0].rstrip("012345") if writes else "", 0.0))
+    def S(name, lo=0, hi=None, step=1, rows=None):
+        width = SCRATCH[name][1][1]
+        hi = width if hi is None else hi
+        ap = T[name][:, lo:hi:step] if rows is None else T[name][rows[0]:rows[1], lo:hi:step]
+        size = 4 if SCRATCH[name][2] in (F32, I32) else 2
+        return (ap, [(name, lo, hi)], len(range(lo, hi, step)), size, SCRATCH[name][0] == "psum")
 
-    def vec(n):
+    def IND(win, off):
+        return (win[0].indirect(off[0]), win[1] + off[1], 16 * off[2], 0, False)
+
+    def ap(x):
+        return x[0] if isinstance(x, tuple) else x
+
+    def do(eng, call, reads, writes, dur, lat=0.0, tok=None):
+        rd = [r for x in reads if isinstance(x, tuple) for r in x[1]]
+        wr = [r for x in writes for r in x[1]]
+        ops.append((eng, call, rd, wr, dur, lat, tok))
+
+    def cost(out, x, double=False, fixed=0.05):
+        if x[3] == 0:
+            return fixed + x[2] * GATH * CYC
+        n = x[2] * (2 if double else 0.5 if out[3] == 2 and x[3] == 2 else 1)
         return CALL + max(64, n) * CYC
 
-    def gat(n):
-        return 0.05 + n * GATH * CYC
+    def tt(out, x, y, op):
+        d = cost(out, x, True) if not (x[4] or y[4]) else CALL + max(64, x[2]) * CYC
+        do("V", lambda: v.tensor_tensor(out[0], x[0], y[0], op), [x, y], [out], d)
 
-    def tt(out, x, y, op, r, w, n):
-        do("V", lambda: v.tensor_tensor(out, x, y, op), r, w, vec(n))
-
-    def ttg(out, x, y, op, r, w, n):
-        do("V", lambda: v.tensor_tensor(out, x, y, op), r, w, gat(n))
-
-    def ts(out, x, s1, s2, op0, op1, r, w, n):
+    def ts(out, x, s1, op0, s2=None, op1=None):
         if op1 is None:
-            do("V", lambda: v.tensor_scalar(out, x, s1, None, op0), r, w, vec(n))
+            do("V", lambda: v.tensor_scalar(out[0], x[0], ap(s1), None, op0), [x, s1], [out], cost(out, x))
         else:
-            do("V", lambda: v.tensor_scalar(out, x, s1, s2, op0, op1), r, w, vec(n))
+            do("V", lambda: v.tensor_scalar(out[0], x[0], ap(s1), ap(s2), op0, op1), [x, s1, s2], [out], cost(out, x))
 
-    def cp(out, x, r, w, n):
-        do("V", lambda: v.tensor_copy(out, x), r, w, vec(n))
+    def cp(out, x):
+        do("V", lambda: v.tensor_copy(out[0], x[0]), [x], [out], cost(out, x))
 
-    def fill(ap, c, w, n):
-        do("V", lambda: v.memset(ap, c), [], w, vec(n))
+    def scan(out, d0, d1, op1):
+        do("V", lambda: v.tensor_tensor_scan(out[0], d0[0], d1[0], 0.0, OP.add, op1), [d0, d1], [out],
+           CALL + max(64, d0[2]) * CYC)
 
-    def act(out, x, r, w, n, acc=None, scale=1.0, bias=0.0, func=AF.Copy):
-        do("A", lambda: a_.activation(out, x, func, bias=bias, scale=scale, accum_out=acc), r, w, vec(n))
+    def fill(out, c):
+        do("V", lambda: v.memset(out[0], c), [], [out], cost(out, out))
 
-    def actg(out, x, r, w, n):
-        do("A", lambda: a_.activation(out, x, AF.Copy), r, w, gat(n) + 0.015)
+    def act(out, x, scale=1.0, bias=0.0, func=AF.Copy, acc=None):
+        d = 0.065 + x[2] * GATH * CYC if x[3] == 0 else CALL + max(64, x[2]) * CYC
+        do("A", lambda: a_.activation(out[0], x[0], func, bias=ap(bias), scale=ap(scale), accum_out=ap(acc)),
+           [x, scale, bias], [out] + ([acc] if acc else []), d)
 
-    def mm(out, l, x, st, sp, r, w, n):
-        do("P", lambda: pe.matmul(out, l, x, st, sp), r, w, max(64, n) * PCYC)
+    def mm(out, l, x, st=True, sp=True):
+        do("P", lambda: pe.matmul(out[0], l[0], x[0], st, sp), [l, x], [out], max(64, x[2]) * PCYC)
 
-    def load(eng, sem, out, x, w, lat):
-        do(eng, lambda: queues[eng].dma_start(out, x).then_inc(T.sem[sem], 16), [], [w], 0.1, lat, (sem, 16))
+    def mms(out, terms, st=True, sp=True):
+        for i, (l, x) in enumerate(terms):
+            mm(out, l, x, st and i == 0, sp and i == len(terms) - 1)
 
-    def store(eng, sem, out, x, r):
-        do(eng, lambda: queues[eng].dma_start(out, x).then_inc(T.sem[sem], 16), r, [], 0.1, 2.0, (sem, 16))
+    def dma(eng, sem, out, x, reads, writes, lat):
+        do(eng, lambda: queues[eng].dma_start(out, x).then_inc(T.sem[sem], 16), reads, writes, 0.1, lat, (sem, 16))
 
-    load("Y", "ld_pk", T.pk_i[:], T.pk[:], "pk_i", 2.0)
-    load("A", "ld_po", T.po_i[:], T.po[:], "po_i", 2.3)
-    load("Y", "ld_dm", T.dm_i[:], T.dm[:], "dm_i", 2.0)
-    load("A", "ld_wt", T.wt_i[:], T.wt[:], "wt_i", 2.0)
-    load("Y", "ld_xt", T.tab[:, 0:2048], T.xt[:], "tab", 3.5)
+    def iota(out, pat, base=0, cm=0):
+        small = SCRATCH[out[1][0][0]][2] != I32
+        do("G", lambda: g.iota(out[0], pat, base, cm, allow_small_or_imprecise_dtypes=small), [], [out],
+           0.13 + 2 * out[2] * CYC)
 
-    def iota(out, pat, base, cm, w, n, small=True):
-        if small:
-            do("G", lambda: g.iota(out, pat, base, cm, allow_small_or_imprecise_dtypes=True), [], w, 0.13 + 2 * n * CYC)
-        else:
-            do("G", lambda: g.iota(out, pat, base, cm), [], w, 0.13 + 2 * n * CYC)
-    iota(T.ip[:], [[0, 1]], 0, 1, ["ip"], 1, False)
-    iota(T.i8[:], [[0, 16], [1, 8]], 0, 0, ["i8"], 128)
-    iota(T.ic[:], [[1, 240]], -112, 0, ["ic"], 240)
-    iota(T.iperm[:], [[16, 8], [-1, 16]], 15, 0, ["iperm"], 128)
-    iota(T.ienc[:], [[128, 16], [16, 8]], 0, 0, ["ienc"], 128)
-    iota(T.cpool[:], [[2, 32], [0, 8]], 0, 0, ["cpool"], 256)
-    iota(T.ipermf[:], [[1, 16], [16, 8]], 0, 0, ["ipermf"], 128)
-    fill(T.wsel[:], 0.0, ["wsel"], 1024)
-    fill(T.kf[:], -KOFF, ["kf"], 1)
-    for j, (op, s) in enumerate([(OP.bitwise_and, 15), (OP.bitwise_and, 7),
-                                 (OP.arith_shift_right, 4), (OP.arith_shift_right, 3)]):
-        ts(T.pint[:, j:j + 1], T.ip[:], s, None, op, None, ["ip"], ["pint%d" % j], 1)
-    cp(T.pcol[:], T.ip[:], ["ip"], ["pcol"], 1)
-    cp(T.pf[:], T.pint[:], ["pint%d" % j for j in range(4)], ["pf"], 4)
-    ic0 = T.ic[:, 112:240]
-    P16, P8, D16, D8 = (T.pf[:, j:j + 1] for j in range(4))
-    PC, EQ = T.pcol[:], OP.is_equal
-    ts(T.mb[:], T.i8[:, 0:8], D16, None, EQ, None, ["i8", "pf"], ["mb"], 8)
-    ts(T.zb[:], T.ic[:], P16, None, EQ, None, ["ic", "pf"], ["zb"], 240)
-    act(T.ones[:], T.ic[:, 0:128], ["ic"], ["ones"], 128, None, 0.0, 1.0)
-    do("G", lambda: g.affine_select(T.eyeb[:], T.ones[:], [[-1, 128]], EQ, 0.0, 0, 1), ["ones"], ["eyeb"], 0.4)
-    ts(T.eye16[:], ic0, PC, None, EQ, None, ["ic", "pcol"], ["eye16"], 128)
-    ts(T.bc[:], T.i8[:, 0:16], 0.0, P8, OP.mult, OP.add, ["i8", "pf"], ["bc"], 16)
-    ts(T.perm16[:], T.iperm[:], PC, None, EQ, None, ["iperm", "pcol"], ["perm16"], 128)
-    selz = ["selz%d" % i for i in range(0, 2048, 240)]
-    for i in range(0, 2048, 240):
-        n = min(240, 2048 - i)
-        act(T.sel[:, i:i + n], T.ic[:, 0:n], ["ic"], ["selz%d" % i], n, None, 0.0)
-    act(T.tab[:, 2080:TW], T.ic[:, 0:16], ["ic"], ["tabz"], 16, None, 0.0)
-    act(T.yp[:, 2048:2080], T.ic[:, 0:32], ["ic"], ["ypz"], 32, None, 0.0)
-    act(T.onesn[:], T.ic[:, 0:128], ["ic"], ["onesn"], 128, None, 0.0, 0.0078125)
-    act(T.cpool[0:64, 0:240], T.ic[0:64, :], ["ic"], ["cpool"], 240, None, 0.0, 4096.0)
-    act(T.cpool[0:64, 240:256], T.ic[0:64, 0:16], ["ic"], ["cpool"], 16, None, 0.0, 4096.0)
-    act(T.m4eye[:], T.eyeb[:], ["eyeb"], ["m4eye"], 128, None, -4.0)
-    ts(T.sel[:, 0:2048:16], T.i8[:], D16, 4096.0, EQ, OP.mult, ["i8", "pf"] + selz, ["sel"], 128)
-    ts(T.enc16[:], T.ienc[:], P16, None, OP.add, None, ["ienc", "pf"], ["enc16"], 128)
-    ts(T.meye16[:], T.eye16[:], -1.0, None, OP.mult, None, ["eye16"], ["meye16"], 64)
-    ts(T.rf[:], T.i8[:], P8, None, EQ, None, ["i8", "pf"], ["rf"], 128)
+    def select(out, x, pat):
+        do("G", lambda: g.affine_select(out[0], x[0], pat[0], OP.is_equal, 0.0, pat[1], -1), [x], [out],
+           0.17 + 2 * out[2] * CYC)
+
+    EQ, MUL, ADD, SUB, MIN, MAX = OP.is_equal, OP.mult, OP.add, OP.subtract, OP.min, OP.max
+
+    for eng, sem, name, lo, hi, src, lat in [
+            ("Y", "ld_dm", "dm_i", 0, 128, T.dm[:], 2.0), ("A", "ld_wt", "wt_i", 0, 1, T.wt[:], 2.0),
+            ("A", "ld_po", "po_i", 0, 256, T.po[:], 2.4), ("Y", "ld_x0", "tab", 0, 1024, T.xt[:, 0:1024], 3.2),
+            ("A", "ld_x1", "tab", 1024, W, T.xt[:, 1024:W], 4.0), ("Y", "ld_pk", "pk_i", 0, 128, T.pk[:], 4.2)]:
+        dma(eng, sem, S(name, lo, hi)[0], src, [], [S(name, lo, hi)], lat)
+    iota(S("ip"), [[0, 1]], 0, 1)
+    iota(S("idiv"), [[1, 8], [0, 16]])
+    iota(S("icol"), [[1, 128]])
+    iota(S("imod"), [[0, 8], [1, 16]])
+    fill(S("ones"), 1.0)
+    select(S("eyeb"), S("ones"), ([[1, 128]], 0))
+    fill(S("fours"), 4.0)
+    for lo, hi in VCH + ACH:
+        select(S("rep4", 16 * lo, 16 * hi), S("fours", 16 * lo, 16 * hi), ([[1, hi - lo], [0, 16]], lo))
+    iota(S("ico"), [[-16, 2], [0, 8], [-1, 16]], 31 - 2048)
+    iota(S("icp"), [[0, 8], [1, 16]], 0, 16)
+    iota(S("ijt"), [[-16, 2], [0, 128]], 31)
+    iota(S("i16q"), [[16, 128]])
+    ts(S("pint", 0, 1), S("ip"), 15, OP.bitwise_and)
+    ts(S("pint", 1, 2), S("ip"), 4, OP.arith_shift_right)
+    cp(S("pf"), S("pint"))
+    P16, D16 = S("pf", 0, 1), S("pf", 1, 2)
+    ts(S("wcol"), S("wt_i"), 2.0, MUL)
+    ts(S("w2b"), S("idiv"), D16, EQ, S("wcol"), MUL)
+    for rows, c in (((0, 32), 64.0), ((32, 64), 33.0 / 32), ((64, 128), 4096.0)):
+        fill(S("ec", rows=rows), c)
+    fill(S("kf"), 0.0)
+    cp(S("d"), S("dm_i"))
+    cp(S("eye16", 0, 128), S("eyeb"))
+    cp(S("eye16", 128, 256), S("eyeb"))
+    cp(S("o16", 0, 128), S("po_i", 0, 256, 2))
+    cp(S("o16", 128, 256), S("po_i", 1, 256, 2))
+    cp(S("c0"), S("pk_i"))
+    for lo in (0, 1024):
+        ts(S("ntab", lo, lo + 1024), S("tab", lo, lo + 1024), -4.0, MUL)
+    ts(S("ntab", W, TW), S("tab", 0, 32), -4.0, MUL)
+    act(S("tab", W, TW), S("tab", 0, 32))
+    act(S("neye"), S("eyeb"), -1.0)
+    act(S("eye5"), S("eyeb"), 5.0)
+    act(S("n4eye"), S("eyeb"), -4.0)
+    act(S("w10b"), S("w2b"), 5.0)
+    act(S("nw2b"), S("w2b"), -1.0)
+    act(S("yp", W, W + 48), S("icol", 0, 48), 0.0, 64.0)
+    act(S("rsp"), S("icol"), 0.0)
+    act(S("rsp", 0, 128, 16), S("icol", 0, 8), 0.0, BIG)
     for j in range(2):
-        ts(T.r256[:, 128 * j:128 * j + 128], T.rf[:], -1.0, None, OP.mult, None, ["rf"], ["r256"], 128)
-    boost[0] = EARLY
-    cp(T.dt_[:], T.dm_i[:], ["dm_i"], ["dt"], 128)
-    ts(T.wcol[:], T.wt_i[:], 2.0, None, OP.mult, None, ["wt_i"], ["wcol"], 1)
-    ts(T.wsel[:, 0:2048:16], T.i8[:], D16, T.wcol[:], EQ, OP.mult, ["i8", "pf", "wcol", "wsel"], ["wsel"], 128)
-    boost[0] = 0.0
-    act(T.tab[:, 2048:2080], T.tab[:, 0:32], ["tab"], ["tabx"], 32)
-    tabk = ["tab", "tabx", "tabz"]
-    win = T.tab[:, 0:TW]
+        act(S("rso", 128 * j, 128 * j + 128), S("rsp"), -1.0)
+    ts(S("g4"), S("icol", 0, 8), D16, EQ, 1024.0, MUL)
+    cp(S("co16"), S("ico"))
+    cp(S("cp16"), S("icp"))
+    cp(S("bc8"), S("icol", 0, 8))
+    cp(S("w2h"), S("w2b"))
+    ts(S("neye16"), S("eyeb"), -1.0, MUL)
+    ts(S("bo16"), S("idiv"), D16, EQ)
+    ts(S("nbo16"), S("bo16"), -1.0, MUL)
+    ts(S("rb16"), S("icol", 0, 8), D16, EQ)
+    ts(S("mask"), S("imod"), P16, EQ)
+    ts(S("enc"), S("i16q"), P16, ADD)
+    ts(S("jt"), S("ijt"), P16, SUB)
+    TAB, NTAB, EYE, EYE16 = S("tab"), S("ntab"), S("eyeb"), S("eye16", 0, 128)
+    for i in range(8):
+        lo, hi = 520 * (i // 2), 520 * (i // 2) + 520
+        act(S("tab5", 2 * lo + i % 2, 2 * hi, 2), S("tab", lo, hi), 2.0, float(i % 2))
+
+    BS, BD, BT, BZ = S("b1", 128, 256), S("b7", 0, 128), S("b7", 128, 256), S("b7", 256, 384)
+    BO, BC, BW = S("b4", 0, 256), S("b5", 384, 512), S("b5", 256, 384)
+    turn = [0]
+
+    def spare():
+        turn[0] += 1
+        return "b%d" % (2 + turn[0] % 2)
+
+    def ybuf(s, lo, hi, step=1):
+        return S("yp", lo, hi, step) if s == 2 else S("yo_", W * s + lo, W * s + hi, step)
 
     def seats_e():
-        for a in range(16):
-            mm(T.b7[:, 128:136], T.wsel[:, 127 * a:127 * a + 128], T.dt_[:, a:128:16], a == 0, a == 15,
-               ["wsel", "dt"], ["B7.e"], 8)
-        act(T.e1[:], T.b7[:, 128:136], ["B7.e"], ["e1"], 8, None, 1.0, EOFF - 1023.0)
-        tt(T.e2[:], T.b7[:, 128:136], T.e1[:], OP.subtract, ["B7.e", "e1"], ["e2"], 8)
-        do("V", lambda: v.tensor_scalar(T.e33[:], T.e2[:].indirect(T.bc[:, 0:4]), 1.0, EOFF + 33.0, OP.mult, OP.add),
-           ["e2", "bc"], ["e33"], gat(64))
-        for i in range(4):
-            act(T.e33w[:, 64 * i:64 * i + 64], T.e33[:], ["e33"], ["e33w%d" % i], 64)
+        act(S("e1"), BS, 1.0, -1056.0)
+        tt(S("e33"), BS, S("e1"), SUB)
 
-    def spread_d(fused=True):
-        for i in range(4):
-            mm(T.b5[:, 128 * i:128 * i + 128], T.eyeb[:], T.dt_[:], True, True, ["eyeb", "dt"], ["B5.d"], 128)
-        if fused:
-            act(T.dt2[:], T.b5[:], ["B5.d", "e33"], ["dt2"], 512)
+    def after_d(lv):
+        mm(BT, S("d"), EYE)
+        act(S("dtr"), BT)
+        ts(S("dec"), S("d"), -1.0, ADD, 4.0, MIN)
+        mm(BZ, EYE, S("dec"), True, False)
+        mm(S("b7", 256, 256 + lv), S("n4eye"), S("d", 0, lv), False, True)
+        act(S("z"), BZ)
 
-    def index(cards, ck, qb, fb, n0, n1, outs, nm):
-        s, n = slice(n0, n1), n1 - n0
-        ek = ["e33w%d" % i for i in range((n + 63) // 64)]
-        cyc = n if ck[0] == "B" else 2 * n
-        if n == 64:
-            tt(qb[:, s], cards, T.e33[:], OP.mult, [ck, "e33"], [nm + "q"], cyc)
-        else:
-            tt(qb[:, s], cards, T.e33w[:, 0:n], OP.mult, [ck] + ek, [nm + "q"], cyc)
-        ts(fb[:, s], qb[:, s], 5, 2047, OP.arith_shift_right, OP.bitwise_and, [nm + "q"], [nm + "f"], n)
-        for out, z, key in outs:
-            ts(out[:, s], fb[:, s], T.kf[:], KOFF + z, OP.add, OP.add, [nm + "f", "kf"], [key], n)
+    def spread():
+        for lo, hi in VCH:
+            b = S(spare(), 0, 16 * (hi - lo))
+            mm(b, S("dtr"), S("rep4", 16 * lo, 16 * hi))
+            act(S("dsp", 16 * lo, 16 * hi), b, -1.0)
 
-    def block(x, y, off, base, pieces, nm, uk):
-        keys = []
-        end = base + pieces[-1][1]
-        for lo, hi in pieces:
-            lo, hi = lo + base, hi + base
-            actg(x[:, lo:hi], win.indirect(off[:, lo // 16:hi // 16]), tabk + [uk], [nm + "x%d" % lo], hi - lo)
-        if end < base + 1024:
-            ttg(y[:, end:base + 1024], win.indirect(off[:, end // 16:(base + 1024) // 16]),
-                T.dt2[:, 0:base + 1024 - end], OP.min, tabk + [uk, "dt2"], [nm + "f%d" % end], base + 1024 - end)
-            keys.append(nm + "f%d" % end)
-        for lo, hi in pieces:
-            lo, hi = lo + base, hi + base
-            tt(y[:, lo:hi], x[:, lo:hi], T.b5[:, 0:hi - lo], OP.min, [nm + "x%d" % lo, "B5.d"], [nm + "y%d" % lo], hi - lo)
-            keys.append(nm + "y%d" % lo)
-        return keys
+    def index(s, cards):
+        lo, hi = 128 * s, 128 * s + 128
+        tt(S("iq", lo, hi), cards, S("e33"), MUL)
+        ts(S("jf", lo, hi), S("iq", lo, hi), 5, OP.arith_shift_right, W - 1, OP.bitwise_and)
+        out = S("iu", lo, hi) if s < 3 else S("mt")
+        ts(out, S("jf", lo, hi), S("kf"), ADD)
 
-    def scores(out, k, const, l, ck, y, base, keys):
-        mm(out, l, const, True, False, ck, [k], 64)
-        for a in range(16):
-            mm(out, T.sel[:, 127 * a:127 * a + 128], y[:, base + a:base + 1024:16], False, a == 15, ["sel"] + keys, [k], 64)
+    def raw(s, lo, hi):
+        return S("xr", W * s + 16 * lo, W * s + 16 * hi)
 
-    def pools(t, share):
-        index(T.b3[:, 0:64], "B3.o", T.oq, T.of, 0, 64, [(T.ou, 0.0, "oua")], "oa")
-        index(T.b3[:, 64:256], "B3.o", T.oq, T.of, 64, 256, [(T.ou, 0.0, "oub")], "ob")
-        for c in range(4):
-            keys = block(T.xo, T.yo_, T.ou, 1024 * c, share[c], "o", "oub" if c else "oua")
-            scores(T.b0[:, 64 * c:64 * c + 64], "B0.s", T.cpool[:, 64 * c:64 * c + 64], T.onesn[:], ["onesn", "cpool"],
-                   T.yo_, 1024 * c, keys)
+    def offs(s, lo, hi):
+        return S("iu", 128 * s + lo, 128 * s + hi)
 
-    def pool_min():
-        act(T.sohi[:], T.b0[:, 128:256], ["B0.s"], ["sohi"], 128)
-        tt(T.p128[:], T.b0[:, 0:128], T.sohi[:], OP.min, ["B0.s", "sohi"], ["p128"], 128)
-        tt(T.p64[:], T.p128[:, 0:64], T.p128[:, 64:128], OP.min, ["p128"], ["p64"], 128)
-        tt(T.p32[:], T.p64[:, 0:32], T.p64[:, 32:64], OP.min, ["p64"], ["p32"], 64)
-        tt(T.p16[:], T.p32[:, 0:16], T.p32[:, 16:32], OP.min, ["p32"], ["p16"], 32)
-        tt(T.omin[:], T.p16[:, 0:8], T.p16[:, 8:16], OP.min, ["p16"], ["omin"], 16)
+    def clip_a(s, lo, hi):
+        b = S(spare(), 0, 16 * (hi - lo))
+        mms(b, [(S("dtr"), S("rep4", 16 * lo, 16 * hi)), (EYE, raw(s, lo, hi))])
+        act(ybuf(s, 16 * lo, 16 * hi), b, func=AF.Relu)
+
+    def scores(s):
+        bank, base = ("b1", 0) if s == 2 else ("b0", 128 * s)
+        if s == 0:
+            mm(S("b0", 0, 256), EYE16, S("co16"), True, False)
+        if s == 2:
+            mm(S("b1", 0, 128), EYE16, S("cp16"), True, False)
+        for k in range(16):
+            mm(S(bank, base + k, base + 128, 16), ybuf(s, k, W, 16), S("g4"), False, s > 0 and k == 15)
+
+    def gathers(s):
+        for i in range(max(len(VCALL[s]), len(ACH))):
+            if i < len(ACH):
+                lo, hi = ACH[i]
+                act(raw(s, lo, hi), IND(TAB, offs(s, lo, hi)), -4.0)
+                clip_a(s, lo, hi)
+            if i < len(VCALL[s]):
+                lo, hi = VCALL[s][i]
+                tt(ybuf(s, 16 * lo, 16 * hi), IND(NTAB, offs(s, lo, hi)), S("dsp", 16 * lo, 16 * hi), MAX)
+        scores(s)
 
     def pool_card(t):
-        actg(T.thr2[:], T.omin[:].indirect(T.bc[:]), ["omin", "bc"], ["thr2"], 256)
-        tt(T.oh[:, 128:384], T.b0[:, 0:256], T.thr2[:], EQ, ["B0.s", "thr2"], ["oho"], 256)
-        tt(T.com[:, 128:384], T.oh[:, 128:384], T.b3[:, 0:256], OP.mult, ["oho", "B3.o"], ["com"], 256)
-        mm(T.b3[:, 0:256], T.eye16[:], T.o16[:], True, False, ["eye16", "o16"], ["B3.o"], 256)
-        for u in range(t):
-            mm(T.b3[:, 0:256], T.eye16[:], T.to16[:, 256 * u:256 * u + 256], False, False, ["eye16", "to%d" % u],
-               ["B3.o"], 256)
-        for j in range(2):
-            mm(T.b6[:, 0:128], T.com[:, 128 + 128 * j:256 + 128 * j], T.eye16[:], j == 0, j == 1, ["com", "eye16"],
-               ["B6.t0"], 128)
-        act(T.tco[:], T.b6[:, 0:128], ["B6.t0"], ["tco"], 128)
-        mm(T.b2[:, 128:256], T.tco[:], T.rf[:], True, False, ["tco", "rf"], ["B2.w"], 512)
-        mm(T.b2[:, 128:256], T.meye16[:], T["c%d" % t][:], False, True, ["meye16", "c%d" % t], ["B2.w"], 128)
-
-    def pack_index(t):
-        boost[0] = 5.0
-        index(T.b4[:, 0:128], "B4.c", T.pq, T.pfc, 0, 128, [(T.pu, 0.0, "pu")], "p")
-        boost[0] = 0.0
-
-    def packs(t, share):
-        all_keys = []
-        for c in range(2):
-            keys = block(T.xp, T.yp, T.pu, 1024 * c, share[4 + c], "p", "pu")
-            scores(T.b1[:, 64 * c:64 * c + 64], "B1.s%d" % c, T.enc16[:, 64 * c:64 * c + 64], T.eye16[:],
-                   ["eye16", "enc16"], T.yp, 1024 * c, keys)
-            all_keys += keys
-            if c == 0:
-                act(T.losb[:], T.b1[:, 0:64], ["B1.s0"], ["losb"], 64)
-        tt(T.w64[:], T.b1[:, 64:128], T.losb[:], OP.max, ["B1.s1", "losb"], ["w64"], 64)
-        tt(T.w32[:], T.w64[:, 0:32], T.w64[:, 32:64], OP.max, ["w64"], ["w32"], 64)
-        tt(T.w16[:], T.w32[:, 0:16], T.w32[:, 16:32], OP.max, ["w32"], ["w16"], 32)
-        tt(T.m1[:], T.w16[:, 0:8], T.w16[:, 8:16], OP.max, ["w16"], ["m1"], 16)
-        return all_keys
-
-    def pack_to_psum(t):
-        mm(T.b4[:, 0:128], T.eye16[:], T["c%d" % t][:], True, True, ["eye16", "c%d" % t], ["B4.c"], 128)
+        scan(S("so"), S("rso"), S("b0", 0, 256), MAX)
+        tt(S("omax"), S("so", 15, 128, 16), S("so", 143, 256, 16), MAX)
+        ts(S("ol"), S("omax"), 31, OP.bitwise_and)
+        cp(S("uo"), IND(S("ol"), S("bc8")))
+        mm(S("b5", 0, 256), S("uo"), S("eye16"))
+        tt(S("oho"), S("b5", 0, 256), S("jt"), EQ)
+        tt(S("como"), S("oho"), BO, MUL)
+        mms(BW, [(S("bo16"), S("como", 0, 128)), (S("bo16"), S("como", 128, 256)), (S("neye16"), S("c%d" % t))])
+        if t < NV - 1:
+            mms(BO, [(EYE16, S("o16"))] + [(EYE16, S("to16", 256 * u, 256 * u + 256)) for u in range(t)], True, False)
 
     def send(t):
         rid, pid, _ = topo.addr(nxt)
@@ -294,171 +291,161 @@ def rank_program(g, core, T, topo):
         for en in topo.engines(core, nxt)[:NENG]:
             m |= 1 << en
         sem = "arr%d" % (t + 1)
-        src, dst = T["n%d" % t][:], T["c%d" % (t + 1)][:]
-        do("G", lambda: g.remote_dma(dst, src, T.sem[sem], T.sem.loc, pid, rid, m), ["n%d" % t], ["c%d" % (t + 1)],
+        src, dst = S("n%d" % t), S("c%d" % (t + 1))
+        do("G", lambda: g.remote_dma(dst[0], src[0], T.sem[sem], T.sem.loc, pid, rid, m), [src], [dst],
            1.0, WIRE, (sem, NENG))
 
-    def exchange(t, ykeys):
+    def less_fall(bank, base, lv, l1, l5, ln):
+        mm(S(bank, base, base + 128), ln, S("dec"), True, False)
+        mm(S(bank, base, base + lv), l5, S("d", 0, lv), False, False)
+        mm(S(bank, base + lv, base + 128), l1, S("d", lv, 128), False, False)
+
+    def exchange(t, lv):
         last = t == NV - 1
-        mo = ["m1", "omin"]
-        tt(T.thi[:], T.m1[:], T.omin[:], OP.max, mo, ["thi"], 16)
-        tt(T.thf[:], T.m1[:], T.omin[:], OP.max, mo, ["thf"], 16)
-        ts(T.offi[:], T.thi[:], 4095, None, OP.bitwise_and, None, ["thi"], ["offi"], 8)
-        cp(T.offu[:], T.offi[:], ["offi"], ["offu"], 8)
-        actg(T.thr[:], T.thf[:].indirect(T.bc[:, 0:8]), ["thf", "bc"], ["thr"], 128)
-        ttg(T.gt[:], T.yp[:].indirect(T.offu[:]), T.dt_[:], OP.is_ge, ykeys + ["ypz", "offu", "dt"], ["gt"], 128)
-        mm(T.b7[:, 0:128], T.eyeb[:], T.dt_[:], True, False, ["eyeb", "dt"], ["B7.d"], 128)
-        mm(T.b7[:, 0:128], T.m4eye[:], T.gt[:], False, True, ["m4eye", "gt"], ["B7.d"], 128)
-        ts(T.dt_[:], T.b7[:, 0:128], 1.0, None, OP.max, None, ["B7.d"], ["dt"], 128)
-        if last:
-            act(T.yd_f[:], T.dt_[:], ["dt"], ["yd_f"], 128)
-            store("Y", "st_yd", T.yd[:], T.yd_f[:], ["yd_f"])
-        tt(T.oh[:, 0:128], T.b1[:, 0:128], T.thr[:], OP.is_ge, ["B1.s0", "B1.s1", "thr"], ["ohc"], 128)
-        tt(T.com[:, 0:128], T.oh[:, 0:128], T.b2[:, 128:256], OP.mult, ["ohc", "B2.w"], ["tuc"], 128)
-        tt(T["n%d" % t][:], T.com[:, 0:128], T.b4[:, 0:128], OP.add, ["tuc", "B4.c"], ["n%d" % t], 128)
+        less_fall("b7", 0, lv, EYE, S("eye5"), S("neye"))
+        scan(S("sp_"), S("rsp"), S("b1", 0, 128), MIN)
         if not last:
-            send(t)
-        mm(T.b6[:, 128:256], T.com[:, 0:128], T.eye16[:], True, True, ["tuc", "eye16"], ["B6.t"], 128)
+            less_fall("b1", 128, lv, S("w2b"), S("w10b"), S("nw2b"))
+            mm(BS, S("ones"), S("ec"), False, False)
+        tt(S("thi"), S("sp_", 15, 128, 16), S("omax"), MIN)
+        ts(S("tl"), S("thi"), 4095, OP.bitwise_and)
+        tt(S("mk"), IND(S("tl"), S("bc8")), S("mask"), MUL)
+        mm(S("b0", 384, 392), S("mk"), S("rb16"))
+        cp(S("offu"), S("b0", 384, 392))
+        tt(S("keep"), IND(S("yp"), S("offu")), S("z"), MIN)
         if not last:
-            mm(T.b2[:, 0:128], T.ones[:], T.oh[:, 0:128], True, True, ["ones", "ohc"], ["B2.k"], 128)
-            act(T.cscr[:], T.b2[:, 0:128], ["B2.k"], ["cnt", "cscr"], 128, T.cnt[:])
-            act(T.kr[:], T.cnt[:], ["cnt"], ["kr"], 1, None, 1.0, KOFF - 15.5)
-            do("A", lambda: a_.activation(T.kf[:], T.kr[:], AF.Identity, bias=T.cnt[:], scale=-1.0), ["kr", "cnt"],
-               ["kf"], vec(1))
+            mm(BS, S("w2h"), S("keep"), False, True)
             seats_e()
-        cp(T.tc16[:], T.b6[:, 128:256], ["B6.t"], ["tc16"], 128)
-        mm(T.b6[:, 256:512], T.tc16[:], T.r256[:], True, True, ["tc16", "r256"], ["B6.d"], 256)
-        to = T.to16[:, 256 * t:256 * t + 256]
-        tt(to, T.oh[:, 128:384], T.b6[:, 256:512], OP.mult, ["oho", "B6.d"], ["to%d" % t], 256)
-        mm(T.b3[:, 0:256], T.eye16[:], to, False, True, ["eye16", "to%d" % t], ["B3.o"], 256)
-        if not last:
-            spread_d(t < NV - 2)
+        mm(BD, EYE16, S("keep"), False, True)
+        cp(S("up"), IND(S("tl"), S("bc8")))
+        mm(S("b6", 0, 128), S("up"), EYE16)
+        tt(S("ohp"), S("b6", 0, 128), S("enc"), EQ)
+        tt(S("comp"), S("ohp"), BW, MUL)
+        for j in range(2):
+            mm(S("b6", 128 + 128 * j, 256 + 128 * j), S("nbo16"), S("comp"))
+        to = S("to16", 256 * t, 256 * t + 256)
+        if last:
+            act(S("yd_f"), BD)
+            dma("A", "st_yd", T.yd[:], T.yd_f[:], [S("yd_f")], [], 2.0)
+            tt(S("yc_f"), S("comp"), BC, ADD)
+            dma("Y", "st_yc", T.yc[:], T.yc_f[:], [S("yc_f")], [], 2.0)
+            tt(to, S("oho"), S("b6", 128, 384), MUL)
+            for j in range(2):
+                tt(S("yo_f", j, 256, 2), S("to16", 256 * t + 128 * j, 256 * t + 128 * j + 128),
+                   S("b4", 128 * j, 128 * j + 128), ADD)
+            dma("Y", "st_yo", T.yo[:], T.yo_f[:], [S("yo_f")], [], 2.0)
+            return
+        tt(S("n%d" % t), S("comp"), BC, ADD)
+        send(t)
+        tt(to, S("oho"), S("b6", 128, 384), MUL)
+        mm(BO, EYE16, to, False, True)
+        mm(S("b0", 256, 384), S("ones"), S("ohp"))
+        act(S("kscr"), S("b0", 256, 384), 1.0, KOFF / 128, AF.Copy, S("kacc"))
+        act(S("kr"), S("kacc"), 1.0, -15.5)
+        act(S("kf"), S("kr"), -1.0, S("kacc"), AF.Identity)
+        act(S("d"), BD)
 
-    Q = [T.q3[:, 128 * i:128 * i + 128] for i in range(3)]
-    RW = [T.rw3[:, 1024 * i:1024 * i + 1024] for i in range(3)]
-    BK = [T.b0, T.b1, T.b2]
-    cp(T.pk16[:], T.pk_i[:], ["pk_i"], ["pk16"], 128)
-    cp(T.poa16[:], T.po_i[:, 0:256:2], ["po_i"], ["poa16"], 128)
-    cp(T.pob16[:], T.po_i[:, 1:256:2], ["po_i"], ["pob16"], 128)
-    boost[0] = EARLY
+    mms(BS, [(S("ones"), S("ec")), (S("w2b"), S("d"))])
     seats_e()
-    boost[0] = 0.0
-    for i, (src, p) in enumerate([("pk16", "perm16"), ("poa16", "eye16"), ("pob16", "eye16")]):
-        mm(T.b0[:, 128 * i:128 * i + 128], T[src][:], T[p][:], True, True, [src, p], ["B0.q%d" % i], 128)
-    cp(T.q3[:], T.b0[:, 0:384], ["B0.q0", "B0.q1", "B0.q2"], ["q3"], 384)
-    for b in range(8):
-        ts(T.rw3[:, b:3072:8], T.q3[:], T.mb[:, b:b + 1], None, OP.mult, None, ["q3", "mb"], ["rw%d" % b], 192)
-    for i, (out, k) in enumerate([(T.b4[:, 0:128], "B4.c"), (T.b3[:, 0:128], "B3.o"), (T.b3[:, 128:256], "B3.o")]):
-        for x in range(8):
-            mm(out, T.zb[:, 112 - 16 * x:240 - 16 * x], T.rw3[:, 1024 * i + 128 * x:1024 * i + 128 * x + 128],
-               x == 0, x == 7, ["zb"] + ["rw%d" % b for b in range(8)], [k], 128)
-    cp(T.c0[:], T.b4[:, 0:128], ["B4.c"], ["c0"], 128)
-    spread_d()
-    pack_index(0)
-    cp(T.o16[:], T.b3[:, 0:256], ["B3.o"], ["o16"], 256)
-
+    mm(BO, EYE16, S("o16"))
     for t in range(NV - 1):
-        share = SHARE
-        pools(t, share)
-        pool_min()
+        after_d(LV)
+        spread()
+        for s in range(2):
+            index(s, S("b4", 128 * s, 128 * s + 128))
+        gathers(0)
+        mm(BC, EYE16, S("c%d" % t))
+        index(2, BC)
+        gathers(1)
         pool_card(t)
-        if t:
-            pack_to_psum(t)
-            pack_index(t)
-        exchange(t, packs(t, share))
+        gathers(2)
+        exchange(t, LV)
 
     t = NV - 1
+    for s in range(2):
+        index(s, S("b4", 128 * s, 128 * s + 128))
+    index(3, S("n0"))
+    ts(S("mz"), S("mt"), 2.0, MUL)
+    ts(S("dlo"), S("d"), -8.0, ADD, 1.0, MAX)
+    ts(S("dhi"), S("d"), 8.0, ADD, 255.0, MIN)
+    mms(S("b6", 0, 128), [(EYE, S("dhi")), (S("neye"), S("dlo"))])
+    fill(S("b0"), 0.0)
+    fill(S("b0", 0, 512, 16), -BIG)
+    pieces = [(s, lo) for s in range(3) for lo in range(0, 128, 32)]
 
-    def chain(off, okey, y, acc, half, out, key):
-        two = key == "cb"
-        for i in range(2 if two else 3):
-            actg(y[:, 512 * i:512 * i + 512], win.indirect(off[:, 32 * i:32 * i + 32]), tabk + [okey], [key + "g%d" % i], 512)
-        ttg(acc[0][:], win.indirect(off[:, 96:128]), y[:, 0:512], OP.max, tabk + [okey, key + "g0"], [key + "0"], 512)
-        if two:
-            ttg(acc[1][:], win.indirect(off[:, 64:96]), acc[0][:], OP.max, tabk + [okey, key + "0"], [key + "1"], 512)
-        for i, b in ((2, T.b6),) if two else ((1, T.b2), (2, T.b6)):
-            bk = ("B2." if i == 1 else "B6.") + key
-            q = i - 1 if two else i
-            mm(b[:], T.eyeb[:], y[:, 512 * q:512 * q + 512], True, True, ["eyeb", key + "g%d" % q], [bk], 512)
-            if i == 1:
-                tt(acc[1][:], acc[0][:], b[:], OP.max, [key + "0", bk], [key + "1"], 512)
-            else:
-                tt(acc[0][:, 0:256], acc[1][:, 0:256], b[:, 0:256], OP.max, [key + "1", bk], [key + "2"], 256)
-                tt(T.b0[:, 0:256], acc[1][:, 256:512], b[:, 256:512], OP.max, [key + "1", bk], ["B0." + key], 256)
-        tt(half[:], acc[0][:, 0:256], T.b0[:, 0:256], OP.max, [key + "2", "B0." + key], [key + "h"], 256)
-        tt(out[0], half[:, 0:128], half[:, 128:256], OP.max, [key + "h"], [out[1]], 256)
-    index(T.n0[:], "n0", T.mq, T.mfc, 0, 128, [(T.mu, 0.0, "mu"), (T.mz, -float(ZC), "mz")], "m")
-    chain(T.mu, "mu", T.yb, [T.acc0, T.acc1], T.bh, (T.b1[:, 0:128], "B1.bm"), "cb")
-    pack_to_psum(t)
-    pack_index(t)
-    tt(T.b4[:, 128:256], T.n0[:], T.b4[:, 0:128], EQ, ["n0", "B4.c"], ["B4.stay"], 128)
-    tt(T.sz[:], T.b4[:, 128:256], T.mz[:], OP.mult, ["B4.stay", "mz"], ["sz"], 128)
-    ts(T.au[:], T.sz[:], float(ZC), None, OP.add, None, ["sz"], ["au"], 128)
-    chain(T.au, "au", T.ya, [T.acc2, T.acc3], T.ah, (T.amax[:], "cam"), "ca")
-    tt(T.up[:], T.amax[:], T.b1[:, 0:128], OP.is_ge, ["cam", "B1.bm"], ["up"], 128)
-    ts(T.b4[:, 384:512], T.up[:], 16.0, -8.0, OP.mult, OP.add, ["up"], ["B4.up8"], 128)
-    tt(T.dsum[:], T.dt_[:], T.b4[:, 384:512], OP.add, ["dt", "B4.up8"], ["dsum"], 128)
-    ts(T.dt_[:], T.dsum[:], 1.0, 255.0, OP.max, OP.min, ["dsum"], ["dt"], 128)
-    spread_d(False)
-    pools(t, [FULL] * 6)
-    pool_min()
-    pool_card(t)
-    exchange(t, packs(t, [FULL] * 6))
-
-    ts(T.permf16[:], T.ipermf[:], PC, None, EQ, None, ["ipermf", "pcol"], ["permf16"], 128)
-    ts(T.prev[:], D8, -1.0, 15.0, OP.mult, OP.add, ["pf"], ["prev"], 1)
-    ts(T.mf[:], T.i8[:, 0:8], P8, None, EQ, None, ["i8", "pf"], ["mf"], 8)
-    ts(T.zfo[:], T.ic[:], D8, None, EQ, None, ["ic", "pf"], ["zfo"], 240)
-    ts(T.zfp[:], T.ic[:], T.prev[:], None, EQ, None, ["ic", "prev"], ["zfp"], 240)
-
-    def seats_to_list(i, src, skey, z, zk, out, ok, dst, dk):
-        k = "B%d.f" % i
-        mm(BK[i][:, 384:512], src, T.permf16[:], True, True, [skey, "permf16"], [k], 128)
-        cp(Q[i], BK[i][:, 384:512], [k], ["q%d" % i], 128)
-        for b in range(8):
-            ts(RW[i][:, 128 * b:128 * b + 128], Q[i], T.mf[:, b:b + 1], None, OP.mult, None, ["q%d" % i, "mf"],
-               ["rx%d%d" % (i, b)], 64)
-        for x in range(8):
-            mm(out, z[:, 112 - 16 * x:240 - 16 * x], RW[i][:, x:1024:8], x == 0, x == 7,
-               [zk] + ["rx%d%d" % (i, b) for b in range(8)], [ok], 128)
-        act(dst, out, [ok], [dk], 128)
-    oe, oek = T.o16[:], "o16"
-    cp(oe, T.b3[:, 0:256], ["B3.o"], [oek], 256)
-    seats_to_list(0, T["n%d" % t][:], "n%d" % t, T.zfp, "zfp", T.b4[:, 0:128], "B4.y", T.yc_f[:], "yc_f")
-    seats_to_list(1, oe[:, 0:128], oek, T.zfo, "zfo", T.b5[:, 0:128], "B5.y", T.yo_f[:, 0:256:2], "yo_f0")
-    seats_to_list(2, oe[:, 128:256], oek, T.zfo, "zfo", T.b7[:, 0:128], "B7.y", T.yo_f[:, 1:256:2], "yo_f1")
-    store("Y", "st_yc", T.yc[:], T.yc_f[:], ["yc_f"])
-    store("Y", "st_yo", T.yo[:], T.yo_f[:], ["yo_f0", "yo_f1"])
+    def gather_raw(i):
+        s, lo = pieces[i]
+        if i < V5RAW:
+            cp(raw(s, lo, lo + 32), IND(NTAB, offs(s, lo, lo + 32)))
+        else:
+            act(raw(s, lo, lo + 32), IND(TAB, offs(s, lo, lo + 32)), -4.0)
+    for i in range(8):
+        gather_raw(i)
+    mm(BC, EYE16, S("c%d" % t))
+    tt(S("b5", 0, 128), S("n0"), S("c%d" % t), EQ)
+    tt(S("mt"), S("b5", 0, 128), S("mz"), ADD)
+    cp(S("au"), S("mt"))
+    index(2, BC)
+    for i in range(4):
+        x, out = IND(S("tab5"), S("au", 32 * i, 32 * i + 32)), S("v5", 512 * i, 512 * i + 512)
+        if i == 0:
+            cp(out, x)
+        else:
+            act(out, x)
+        scan(S("s5", 512 * i, 512 * i + 512), S("b0"), out, MAX)
+    for i in range(8, 12):
+        gather_raw(i)
+    cp(S("vi"), S("s5", 15, W, 16))
+    ts(S("vu"), S("vi"), 1, OP.bitwise_and)
+    tt(S("ud"), S("vu"), S("b6", 0, 128), MUL)
+    mms(BT, [(S("dlo"), EYE), (S("ud"), EYE)])
+    act(S("ndtr"), BT, -1.0)
+    act(S("dtr"), BT)
+    mms(BD, [(EYE, S("dlo")), (EYE, S("ud"))])
+    act(S("d"), BD)
+    ts(S("dec"), S("d"), -1.0, ADD, 4.0, MIN)
+    mm(BZ, EYE, S("dec"), True, False)
+    mm(S("b7", 256, 256 + LV5), S("n4eye"), S("d", 0, LV5), False, True)
+    act(S("z"), BZ)
+    for lo, bank in ((0, "b1"), (32, "b6")):
+        mm(S(bank), S("ndtr"), S("rep4", 16 * lo, 16 * lo + 512))
+    for lo, bank in ((0, "b1"), (32, "b6")):
+        for s in range(3):
+            tt(ybuf(s, 16 * lo, 16 * lo + 512), raw(s, lo, lo + 32), S(bank), MAX)
+    for s in range(3):
+        for lo in range(LV5, 128, 32):
+            clip_a(s, lo, lo + 32)
+        scores(s)
+        if s == 1:
+            pool_card(t)
+    exchange(t, LV5)
 
     n = len(ops)
     preds = [{} for _ in range(n)]
-    lastw, readers, bankacc = {}, {}, {}
+    seen, bankacc = {}, {}
     for i, (eng, call, reads, writes, dur, lat, tok) in enumerate(ops):
         def edge(j, wait, i=i):
             if j != i:
                 preds[i][j] = preds[i].get(j, False) or wait
-        for k in reads:
-            if k in lastw:
-                edge(lastw[k], True)
-        for k in writes:
-            if k in lastw:
-                edge(lastw[k], ops[lastw[k]][0] != eng)
-            for j in readers.get(k, []):
-                edge(j, ops[j][0] != eng or ops[j][6] is not None)
-        for k in sorted({k[:2] for k in reads + writes if k[0] == "B"}):
-            turn = bankacc.setdefault(k, [eng, [], []])
-            if turn[0] != eng:
-                turn[0], turn[1], turn[2] = eng, turn[2], []
-            for j in turn[1]:
+        for wr, ranges in ((False, reads), (True, writes)):
+            for name, lo, hi in ranges:
+                for l2, h2, j, w2 in seen.get(name, []):
+                    if l2 < hi and lo < h2 and (wr or w2):
+                        edge(j, (w2 and not (wr and eng == "P")) or ops[j][0] != eng or ops[j][6] is not None)
+        for k in sorted({r[0] for r in reads + writes if SCRATCH[r[0]][0] == "psum"}):
+            tn = bankacc.setdefault(k, [eng, [], []])
+            if tn[0] != eng:
+                tn[0], tn[1], tn[2] = eng, tn[2], []
+            for j in tn[1]:
                 edge(j, True)
-            if eng == "P" and turn[2]:
-                edge(turn[2][-1], False)
-            turn[2].append(i)
-        for k in reads:
-            readers.setdefault(k, []).append(i)
-        for k in writes:
-            lastw[k] = i
-            readers[k] = []
+            if eng == "P" and tn[2]:
+                edge(tn[2][-1], False)
+            tn[2].append(i)
+        for name, lo, hi in writes:
+            seen[name] = [e for e in seen.get(name, []) if not (lo <= e[0] and e[1] <= hi and ops[e[2]][0] != eng)]
+            seen[name] = [e for e in seen[name] if not (lo == e[0] and e[1] == hi)] + [(lo, hi, i, True)]
+        for name, lo, hi in reads:
+            seen.setdefault(name, []).append((lo, hi, i, False))
     succs = [[] for _ in range(n)]
     for i in range(n):
         for j in preds[i]:
@@ -470,6 +457,8 @@ def rank_program(g, core, T, topo):
         for s in succs[i]:
             best = max(best, prio[s] + (own + HOP if preds[s][i] else ops[i][4]))
         prio[i] = max(best, own)
+    for i in range(n):
+        prio[i] += BOOST.get(ops[i][3][0][0] if ops[i][3] else "", 0.0)
 
     left = [len(p) for p in preds]
     est = [0.0] * n
@@ -484,7 +473,7 @@ def rank_program(g, core, T, topo):
         for e in queues:
             if ready[e]:
                 st = max(free[e], min(est[i] for i in ready[e]))
-                i = max((i for i in ready[e] if est[i] <= st + 1e-9), key=lambda i: (prio[i] + boosts[i], -i))
+                i = max((i for i in ready[e] if est[i] <= st + 1e-9), key=lambda i: (prio[i], -i))
                 if pick is None or st < pick[0]:
                     pick = (st, e, i)
         st, e, i = pick

@@ -8,11 +8,11 @@ W = 2048
 TW = 2080
 KOFF = 4128.0
 BIG = 67108864.0
-LV = 72
+LV = 80
 VCH = [(0, 32), (32, 64), (64, LV)]
 VCALL = [[(0, 32), (32, LV)], [(0, LV)], [(0, LV)]]
-ACH = [(LV, 100), (100, 128)]
-LV5 = 64
+ACH = [(LV, LV // 4 * 2 + 64), (LV // 4 * 2 + 64, 128)]
+LV5 = 96
 V5RAW = 2
 
 
@@ -57,7 +57,7 @@ STORES = ["st_yc", "st_yo", "st_yd"]
 ARR = ["arr%d" % t for t in range(1, NV)]
 SEMAPHORES = ["sv", "sa", "sp", "sg", "loc"] + LOADS + STORES + ARR
 
-CYC, PCYC, CALL, HOP, GATH, WIRE = 0.00091, 0.0007, 0.05, 0.06, 1.5, 3.5
+CYC, PCYC, CALL, HOP, GATH, WIRE = 0.00091, 0.0008, 0.05, 0.06, 1.5, 3.5
 BOOST = {"tab5": -30.0}
 
 
@@ -206,7 +206,7 @@ def rank_program(g, core, T, topo):
         lo, hi = 520 * (i // 2), 520 * (i // 2) + 520
         act(S("tab5", 2 * lo + i % 2, 2 * hi, 2), S("tab", lo, hi), 2.0, float(i % 2))
 
-    BS, BD, BT, BZ = S("b1", 128, 256), S("b7", 0, 128), S("b7", 128, 256), S("b7", 256, 384)
+    BS, BD, BT, BZ = S("b0", 256, 384), S("b7", 0, 128), S("b7", 128, 256), S("b7", 256, 384)
     BO, BC, BW = S("b4", 0, 256), S("b5", 384, 512), S("b5", 256, 384)
     turn = [0]
 
@@ -222,8 +222,6 @@ def rank_program(g, core, T, topo):
         tt(S("e33"), BS, S("e1"), SUB)
 
     def after_d(lv):
-        mm(BT, S("d"), EYE)
-        act(S("dtr"), BT)
         ts(S("dec"), S("d"), -1.0, ADD, 4.0, MIN)
         mm(BZ, EYE, S("dec"), True, False)
         mm(S("b7", 256, 256 + lv), S("n4eye"), S("d", 0, lv), False, True)
@@ -248,9 +246,9 @@ def rank_program(g, core, T, topo):
     def offs(s, lo, hi):
         return S("iu", 128 * s + lo, 128 * s + hi)
 
-    def clip_a(s, lo, hi):
-        b = S(spare(), 0, 16 * (hi - lo))
-        mms(b, [(S("dtr"), S("rep4", 16 * lo, 16 * hi)), (EYE, raw(s, lo, hi))])
+    def clip_a(s, lo, hi, bank=None):
+        b = S(bank or spare(), 0, 16 * (hi - lo))
+        mms(b, [(S("dtr"), S("rep4", 16 * lo, 16 * hi)), (EYE, raw(s, lo, hi))][::-1 if bank else 1])
         act(ybuf(s, 16 * lo, 16 * hi), b, func=AF.Relu)
 
     def scores(s):
@@ -302,21 +300,29 @@ def rank_program(g, core, T, topo):
 
     def exchange(t, lv):
         last = t == NV - 1
-        less_fall("b7", 0, lv, EYE, S("eye5"), S("neye"))
-        scan(S("sp_"), S("rsp"), S("b1", 0, 128), MIN)
-        if not last:
-            less_fall("b1", 128, lv, S("w2b"), S("w10b"), S("nw2b"))
+        if last:
+            less_fall("b7", 0, lv, EYE, S("eye5"), S("neye"))
+        else:
+            mms(BT, [(S("dec"), S("neye")), (S("d"), EYE)], True, False)
+            mm(S("b7", 128, 256, rows=(0, lv)), S("d", 0, lv), S("rep4", 0, W, 16), False, False)
+            less_fall("b0", 256, lv, S("w2b"), S("w10b"), S("nw2b"))
             mm(BS, S("ones"), S("ec"), False, False)
+        scan(S("sp_"), S("rsp"), S("b1", 0, 128), MIN)
         tt(S("thi"), S("sp_", 15, 128, 16), S("omax"), MIN)
         ts(S("tl"), S("thi"), 4095, OP.bitwise_and)
         tt(S("mk"), IND(S("tl"), S("bc8")), S("mask"), MUL)
-        mm(S("b0", 384, 392), S("mk"), S("rb16"))
-        cp(S("offu"), S("b0", 384, 392))
+        mm(S("b1", 128, 136), S("mk"), S("rb16"))
+        cp(S("offu"), S("b1", 128, 136))
         tt(S("keep"), IND(S("yp"), S("offu")), S("z"), MIN)
         if not last:
             mm(BS, S("w2h"), S("keep"), False, True)
             seats_e()
-        mm(BD, EYE16, S("keep"), False, True)
+            mm(BT, S("keep"), EYE16, False, True)
+            act(S("dtr"), BT)
+            mm(BD, S("dtr"), EYE)
+            act(S("d"), BD)
+        else:
+            mm(BD, EYE16, S("keep"), False, True)
         cp(S("up"), IND(S("tl"), S("bc8")))
         mm(S("b6", 0, 128), S("up"), EYE16)
         tt(S("ohp"), S("b6", 0, 128), S("enc"), EQ)
@@ -339,15 +345,16 @@ def rank_program(g, core, T, topo):
         send(t)
         tt(to, S("oho"), S("b6", 128, 384), MUL)
         mm(BO, EYE16, to, False, True)
-        mm(S("b0", 256, 384), S("ones"), S("ohp"))
-        act(S("kscr"), S("b0", 256, 384), 1.0, KOFF / 128, AF.Copy, S("kacc"))
+        mm(S("b1", 256, 384), S("ones"), S("ohp"))
+        act(S("kscr"), S("b1", 256, 384), 1.0, KOFF / 128, AF.Copy, S("kacc"))
         act(S("kr"), S("kacc"), 1.0, -15.5)
         act(S("kf"), S("kr"), -1.0, S("kacc"), AF.Identity)
-        act(S("d"), BD)
 
     mms(BS, [(S("ones"), S("ec")), (S("w2b"), S("d"))])
     seats_e()
     mm(BO, EYE16, S("o16"))
+    mm(BT, S("d"), EYE)
+    act(S("dtr"), BT)
     for t in range(NV - 1):
         after_d(LV)
         spread()
@@ -369,8 +376,8 @@ def rank_program(g, core, T, topo):
     ts(S("dlo"), S("d"), -8.0, ADD, 1.0, MAX)
     ts(S("dhi"), S("d"), 8.0, ADD, 255.0, MIN)
     mms(S("b6", 0, 128), [(EYE, S("dhi")), (S("neye"), S("dlo"))])
-    fill(S("b0"), 0.0)
-    fill(S("b0", 0, 512, 16), -BIG)
+    for j in range(2):
+        act(S("b0", 256 * j, 256 * j + 256), S("rso"))
     pieces = [(s, lo) for s in range(3) for lo in range(0, 128, 32)]
 
     def gather_raw(i):
@@ -407,14 +414,13 @@ def rank_program(g, core, T, topo):
     mm(BZ, EYE, S("dec"), True, False)
     mm(S("b7", 256, 256 + LV5), S("n4eye"), S("d", 0, LV5), False, True)
     act(S("z"), BZ)
-    for lo, bank in ((0, "b1"), (32, "b6")):
+    held = ((0, "b1"), (32, "b6"), (64, "b2"))
+    for lo, bank in held:
         mm(S(bank), S("ndtr"), S("rep4", 16 * lo, 16 * lo + 512))
-    for lo, bank in ((0, "b1"), (32, "b6")):
-        for s in range(3):
-            tt(ybuf(s, 16 * lo, 16 * lo + 512), raw(s, lo, lo + 32), S(bank), MAX)
     for s in range(3):
-        for lo in range(LV5, 128, 32):
-            clip_a(s, lo, lo + 32)
+        for lo, bank in held:
+            tt(ybuf(s, 16 * lo, 16 * lo + 512), raw(s, lo, lo + 32), S(bank), MAX)
+        clip_a(s, LV5, 128, "b3")
         scores(s)
         if s == 1:
             pool_card(t)

from concourse.bass import DstId, RemoteDMATransfer
from concourse.mybir import dt, AluOpType, AxisListType, ActivationFunctionType

OP = AluOpType
AF = ActivationFunctionType
NV = 6
W = 2048
TW = 2080
KOFF = 4128.0
BIG = 67108864.0
LV = 80
VCH = [(0, 32), (32, 64), (64, LV)]
VCALL = [[(0, 32), (32, LV)], [(0, LV)], [(0, LV)]]
ACH = [(LV, LV // 4 * 2 + 64), (LV // 4 * 2 + 64, 128)]
LV5 = 96
V5RAW = 2


def sb(n, d):
    return ("sbuf", [128, n], d)


F32, B16, F16, I32, U16 = "float32", "bfloat16", "float16", "int32", "uint16"
SCRATCH = {
    "pk_i": sb(128, I32), "po_i": sb(256, I32), "dm_i": sb(128, I32), "wt_i": sb(1, I32),
    "tab": sb(TW, B16), "ntab": sb(TW, B16), "tab5": sb(2 * TW, F32),
    "ip": sb(1, I32), "pint": sb(2, I32), "pf": sb(2, F32), "icol": sb(128, F32), "idiv": sb(128, F32),
    "imod": sb(128, F32), "i16q": sb(128, F32), "icp": sb(128, F32), "ico": sb(256, F32), "ijt": sb(256, F32),
    "fours": sb(W, B16), "rep4": sb(W, B16), "ones": sb(128, B16), "eyeb": sb(128, B16), "neye": sb(128, B16),
    "eye5": sb(128, B16), "n4eye": sb(128, B16), "eye16": sb(256, F16), "neye16": sb(128, F16),
    "bo16": sb(128, F16), "nbo16": sb(128, F16), "g4": sb(8, B16), "rb16": sb(8, F16), "bc8": sb(8, U16),
    "mask": sb(128, F32), "enc": sb(128, F32), "jt": sb(256, F32), "cp16": sb(128, F16), "co16": sb(256, F16),
    "rsp": sb(128, F32), "rso": sb(256, F32), "ec": sb(128, B16),
    "wcol": sb(1, F32), "w2b": sb(128, B16), "w10b": sb(128, B16), "nw2b": sb(128, B16), "w2h": sb(128, F16),
    "o16": sb(256, F16), "to16": sb(256 * NV, F16),
    "d": sb(128, B16), "dtr": sb(128, B16), "ndtr": sb(128, B16), "dec": sb(128, B16), "z": sb(128, F32),
    "dsp": sb(16 * LV, B16), "e1": sb(128, B16), "e33": sb(128, F32),
    "kacc": sb(1, F32), "kr": sb(1, B16), "kf": sb(1, F32), "kscr": sb(128, F32),
    "iq": sb(512, I32), "jf": sb(512, I32), "iu": sb(384, U16), "mz": sb(128, F32), "mt": sb(128, F32),
    "au": sb(128, U16),
    "xr": sb(3 * W, B16), "yo_": sb(2 * W, B16), "yp": sb(W + 48, B16),
    "so": sb(256, F32), "sp_": sb(128, F32), "omax": sb(8, I32), "ol": sb(8, I32), "thi": sb(8, I32),
    "tl": sb(8, I32), "uo": sb(128, F16), "up": sb(128, F16), "mk": sb(128, F16), "offu": sb(8, U16),
    "oho": sb(256, B16), "como": sb(256, F16), "ohp": sb(128, B16), "comp": sb(128, F16), "keep": sb(128, F16),
    "v5": sb(W, F32), "s5": sb(W, F32), "vi": sb(128, I32), "vu": sb(128, I32), "dlo": sb(128, B16),
    "dhi": sb(128, B16), "ud": sb(128, B16),
    "yc_f": sb(128, F32), "yo_f": sb(256, F32), "yd_f": sb(128, F32),
}
for _t in range(NV):
    SCRATCH["c%d" % _t] = sb(128, F16)
    SCRATCH["n%d" % _t] = sb(128, F16)
for _b in range(8):
    SCRATCH["b%d" % _b] = ("psum", [128, 512], F32)

LOADS = ["ld_dm", "ld_wt", "ld_po", "ld_x0", "ld_x1", "ld_pk"]
STORES = ["st_yc", "st_yo", "st_yd"]
ARR = ["arr%d" % t for t in range(1, NV)]
SEMAPHORES = ["sv", "sa", "sp", "sg", "loc"] + LOADS + STORES + ARR

CYC, PCYC, CALL, HOP, GATH, WIRE = 0.00091, 0.0008, 0.05, 0.06, 1.5, 3.5
BOOST = {"tab5": -30.0}


def rank_program(g, core, T, topo):
    rank = T.rank_of(core)
    if rank is None:
        return
    nxt = T.cores[(rank + 1) % len(T.cores)]
    NENG = 8
    queues = {"V": g.vector, "A": g.scalar, "P": g.tensor, "G": g, "Y": g.sync}
    counters = {"V": "sv", "A": "sa", "P": "sp", "G": "sg"}
    v, a_, pe = g.vector, g.scalar, g.tensor
    ops = []

    def S(name, lo=0, hi=None, step=1, rows=None):
        width = SCRATCH[name][1][1]
        hi = width if hi is None else hi
        ap = T[name][:, lo:hi:step] if rows is None else T[name][rows[0]:rows[1], lo:hi:step]
        size = 4 if SCRATCH[name][2] in (F32, I32) else 2
        return (ap, [(name, lo, hi)], len(range(lo, hi, step)), size, SCRATCH[name][0] == "psum")

    def IND(win, off):
        return (win[0].indirect(off[0]), win[1] + off[1], 16 * off[2], 0, False)

    def ap(x):
        return x[0] if isinstance(x, tuple) else x

    def do(eng, call, reads, writes, dur, lat=0.0, tok=None):
        rd = [r for x in reads if isinstance(x, tuple) for r in x[1]]
        wr = [r for x in writes for r in x[1]]
        ops.append((eng, call, rd, wr, dur, lat, tok))

    def cost(out, x, double=False, fixed=0.05):
        if x[3] == 0:
            return fixed + x[2] * GATH * CYC
        n = x[2] * (2 if double else 0.5 if out[3] == 2 and x[3] == 2 else 1)
        return CALL + max(64, n) * CYC

    def tt(out, x, y, op):
        d = cost(out, x, True) if not (x[4] or y[4]) else CALL + max(64, x[2]) * CYC
        do("V", lambda: v.tensor_tensor(out[0], x[0], y[0], op), [x, y], [out], d)

    def ts(out, x, s1, op0, s2=None, op1=None):
        if op1 is None:
            do("V", lambda: v.tensor_scalar(out[0], x[0], ap(s1), None, op0), [x, s1], [out], cost(out, x))
        else:
            do("V", lambda: v.tensor_scalar(out[0], x[0], ap(s1), ap(s2), op0, op1), [x, s1, s2], [out], cost(out, x))

    def cp(out, x):
        do("V", lambda: v.tensor_copy(out[0], x[0]), [x], [out], cost(out, x))

    def scan(out, d0, d1, op1):
        do("V", lambda: v.tensor_tensor_scan(out[0], d0[0], d1[0], 0.0, OP.add, op1), [d0, d1], [out],
           CALL + max(64, d0[2]) * CYC)

    def fill(out, c):
        do("V", lambda: v.memset(out[0], c), [], [out], cost(out, out))

    def act(out, x, scale=1.0, bias=0.0, func=AF.Copy, acc=None):
        d = 0.065 + x[2] * GATH * CYC if x[3] == 0 else CALL + max(64, x[2]) * CYC
        do("A", lambda: a_.activation(out[0], x[0], func, bias=ap(bias), scale=ap(scale), accum_out=ap(acc)),
           [x, scale, bias], [out] + ([acc] if acc else []), d)

    def mm(out, l, x, st=True, sp=True):
        do("P", lambda: pe.matmul(out[0], l[0], x[0], st, sp), [l, x], [out], max(64, x[2]) * PCYC)

    def mms(out, terms, st=True, sp=True):
        for i, (l, x) in enumerate(terms):
            mm(out, l, x, st and i == 0, sp and i == len(terms) - 1)

    def dma(eng, sem, out, x, reads, writes, lat):
        do(eng, lambda: queues[eng].dma_start(out, x).then_inc(T.sem[sem], 16), reads, writes, 0.1, lat, (sem, 16))

    def iota(out, pat, base=0, cm=0):
        small = SCRATCH[out[1][0][0]][2] != I32
        do("G", lambda: g.iota(out[0], pat, base, cm, allow_small_or_imprecise_dtypes=small), [], [out],
           0.13 + 2 * out[2] * CYC)

    def select(out, x, pat):
        do("G", lambda: g.affine_select(out[0], x[0], pat[0], OP.is_equal, 0.0, pat[1], -1), [x], [out],
           0.17 + 2 * out[2] * CYC)

    EQ, MUL, ADD, SUB, MIN, MAX = OP.is_equal, OP.mult, OP.add, OP.subtract, OP.min, OP.max

    for eng, sem, name, lo, hi, src, lat in [
            ("Y", "ld_dm", "dm_i", 0, 128, T.dm[:], 2.0), ("A", "ld_wt", "wt_i", 0, 1, T.wt[:], 2.0),
            ("A", "ld_po", "po_i", 0, 256, T.po[:], 2.4), ("Y", "ld_x0", "tab", 0, 1024, T.xt[:, 0:1024], 3.2),
            ("A", "ld_x1", "tab", 1024, W, T.xt[:, 1024:W], 4.0), ("Y", "ld_pk", "pk_i", 0, 128, T.pk[:], 4.2)]:
        dma(eng, sem, S(name, lo, hi)[0], src, [], [S(name, lo, hi)], lat)
    iota(S("ip"), [[0, 1]], 0, 1)
    iota(S("idiv"), [[1, 8], [0, 16]])
    iota(S("icol"), [[1, 128]])
    iota(S("imod"), [[0, 8], [1, 16]])
    fill(S("ones"), 1.0)
    select(S("eyeb"), S("ones"), ([[1, 128]], 0))
    fill(S("fours"), 4.0)
    for lo, hi in VCH + ACH:
        select(S("rep4", 16 * lo, 16 * hi), S("fours", 16 * lo, 16 * hi), ([[1, hi - lo], [0, 16]], lo))
    iota(S("ico"), [[-16, 2], [0, 8], [-1, 16]], 31 - 2048)
    iota(S("icp"), [[0, 8], [1, 16]], 0, 16)
    iota(S("ijt"), [[-16, 2], [0, 128]], 31)
    iota(S("i16q"), [[16, 128]])
    ts(S("pint", 0, 1), S("ip"), 15, OP.bitwise_and)
    ts(S("pint", 1, 2), S("ip"), 4, OP.arith_shift_right)
    cp(S("pf"), S("pint"))
    P16, D16 = S("pf", 0, 1), S("pf", 1, 2)
    ts(S("wcol"), S("wt_i"), 2.0, MUL)
    ts(S("w2b"), S("idiv"), D16, EQ, S("wcol"), MUL)
    for rows, c in (((0, 32), 64.0), ((32, 64), 33.0 / 32), ((64, 128), 4096.0)):
        fill(S("ec", rows=rows), c)
    fill(S("kf"), 0.0)
    cp(S("d"), S("dm_i"))
    cp(S("eye16", 0, 128), S("eyeb"))
    cp(S("eye16", 128, 256), S("eyeb"))
    cp(S("o16", 0, 128), S("po_i", 0, 256, 2))
    cp(S("o16", 128, 256), S("po_i", 1, 256, 2))
    cp(S("c0"), S("pk_i"))
    for lo in (0, 1024):
        ts(S("ntab", lo, lo + 1024), S("tab", lo, lo + 1024), -4.0, MUL)
    ts(S("ntab", W, TW), S("tab", 0, 32), -4.0, MUL)
    act(S("tab", W, TW), S("tab", 0, 32))
    act(S("neye"), S("eyeb"), -1.0)
    act(S("eye5"), S("eyeb"), 5.0)
    act(S("n4eye"), S("eyeb"), -4.0)
    act(S("w10b"), S("w2b"), 5.0)
    act(S("nw2b"), S("w2b"), -1.0)
    act(S("yp", W, W + 48), S("icol", 0, 48), 0.0, 64.0)
    act(S("rsp"), S("icol"), 0.0)
    act(S("rsp", 0, 128, 16), S("icol", 0, 8), 0.0, BIG)
    for j in range(2):
        act(S("rso", 128 * j, 128 * j + 128), S("rsp"), -1.0)
    ts(S("g4"), S("icol", 0, 8), D16, EQ, 1024.0, MUL)
    cp(S("co16"), S("ico"))
    cp(S("cp16"), S("icp"))
    cp(S("bc8"), S("icol", 0, 8))
    cp(S("w2h"), S("w2b"))
    ts(S("neye16"), S("eyeb"), -1.0, MUL)
    ts(S("bo16"), S("idiv"), D16, EQ)
    ts(S("nbo16"), S("bo16"), -1.0, MUL)
    ts(S("rb16"), S("icol", 0, 8), D16, EQ)
    ts(S("mask"), S("imod"), P16, EQ)
    ts(S("enc"), S("i16q"), P16, ADD)
    ts(S("jt"), S("ijt"), P16, SUB)
    TAB, NTAB, EYE, EYE16 = S("tab"), S("ntab"), S("eyeb"), S("eye16", 0, 128)
    for i in range(8):
        lo, hi = 520 * (i // 2), 520 * (i // 2) + 520
        act(S("tab5", 2 * lo + i % 2, 2 * hi, 2), S("tab", lo, hi), 2.0, float(i % 2))

    BS, BD, BT, BZ = S("b0", 256, 384), S("b7", 0, 128), S("b7", 128, 256), S("b7", 256, 384)
    BO, BC, BW = S("b4", 0, 256), S("b5", 384, 512), S("b5", 256, 384)
    turn = [0]

    def spare():
        turn[0] += 1
        return "b%d" % (2 + turn[0] % 2)

    def ybuf(s, lo, hi, step=1):
        return S("yp", lo, hi, step) if s == 2 else S("yo_", W * s + lo, W * s + hi, step)

    def seats_e():
        act(S("e1"), BS, 1.0, -1056.0)
        tt(S("e33"), BS, S("e1"), SUB)

    def after_d(lv):
        ts(S("dec"), S("d"), -1.0, ADD, 4.0, MIN)
        mm(BZ, EYE, S("dec"), True, False)
        mm(S("b7", 256, 256 + lv), S("n4eye"), S("d", 0, lv), False, True)
        act(S("z"), BZ)

    def spread():
        for lo, hi in VCH:
            b = S(spare(), 0, 16 * (hi - lo))
            mm(b, S("dtr"), S("rep4", 16 * lo, 16 * hi))
            act(S("dsp", 16 * lo, 16 * hi), b, -1.0)

    def index(s, cards):
        lo, hi = 128 * s, 128 * s + 128
        tt(S("iq", lo, hi), cards, S("e33"), MUL)
        ts(S("jf", lo, hi), S("iq", lo, hi), 5, OP.arith_shift_right, W - 1, OP.bitwise_and)
        out = S("iu", lo, hi) if s < 3 else S("mt")
        ts(out, S("jf", lo, hi), S("kf"), ADD)

    def raw(s, lo, hi):
        return S("xr", W * s + 16 * lo, W * s + 16 * hi)

    def offs(s, lo, hi):
        return S("iu", 128 * s + lo, 128 * s + hi)

    def clip_a(s, lo, hi, bank=None):
        b = S(bank or spare(), 0, 16 * (hi - lo))
        mms(b, [(S("dtr"), S("rep4", 16 * lo, 16 * hi)), (EYE, raw(s, lo, hi))][::-1 if bank else 1])
        act(ybuf(s, 16 * lo, 16 * hi), b, func=AF.Relu)

    def scores(s):
        bank, base = ("b1", 0) if s == 2 else ("b0", 128 * s)
        if s == 0:
            mm(S("b0", 0, 256), EYE16, S("co16"), True, False)
        if s == 2:
            mm(S("b1", 0, 128), EYE16, S("cp16"), True, False)
        for k in range(16):
            mm(S(bank, base + k, base + 128, 16), ybuf(s, k, W, 16), S("g4"), False, s > 0 and k == 15)

    def gathers(s):
        for i in range(max(len(VCALL[s]), len(ACH))):
            if i < len(ACH):
                lo, hi = ACH[i]
                act(raw(s, lo, hi), IND(TAB, offs(s, lo, hi)), -4.0)
                clip_a(s, lo, hi)
            if i < len(VCALL[s]):
                lo, hi = VCALL[s][i]
                tt(ybuf(s, 16 * lo, 16 * hi), IND(NTAB, offs(s, lo, hi)), S("dsp", 16 * lo, 16 * hi), MAX)
        scores(s)

    def pool_card(t):
        scan(S("so"), S("rso"), S("b0", 0, 256), MAX)
        tt(S("omax"), S("so", 15, 128, 16), S("so", 143, 256, 16), MAX)
        ts(S("ol"), S("omax"), 31, OP.bitwise_and)
        cp(S("uo"), IND(S("ol"), S("bc8")))
        mm(S("b5", 0, 256), S("uo"), S("eye16"))
        tt(S("oho"), S("b5", 0, 256), S("jt"), EQ)
        tt(S("como"), S("oho"), BO, MUL)
        mms(BW, [(S("bo16"), S("como", 0, 128)), (S("bo16"), S("como", 128, 256)), (S("neye16"), S("c%d" % t))])
        if t < NV - 1:
            mms(BO, [(EYE16, S("o16"))] + [(EYE16, S("to16", 256 * u, 256 * u + 256)) for u in range(t)], True, False)

    def send(t):
        rid, pid, _ = topo.addr(nxt)
        m = 0
        for en in topo.engines(core, nxt)[:NENG]:
            m |= 1 << en
        sem = "arr%d" % (t + 1)
        src, dst = S("n%d" % t), S("c%d" % (t + 1))
        do("G", lambda: g.remote_dma(dst[0], src[0], T.sem[sem], T.sem.loc, pid, rid, m), [src], [dst],
           1.0, WIRE, (sem, NENG))

    def less_fall(bank, base, lv, l1, l5, ln):
        mm(S(bank, base, base + 128), ln, S("dec"), True, False)
        mm(S(bank, base, base + lv), l5, S("d", 0, lv), False, False)
        mm(S(bank, base + lv, base + 128), l1, S("d", lv, 128), False, False)

    def exchange(t, lv):
        last = t == NV - 1
        if last:
            less_fall("b7", 0, lv, EYE, S("eye5"), S("neye"))
        else:
            mms(BT, [(S("dec"), S("neye")), (S("d"), EYE)], True, False)
            mm(S("b7", 128, 256, rows=(0, lv)), S("d", 0, lv), S("rep4", 0, W, 16), False, False)
            less_fall("b0", 256, lv, S("w2b"), S("w10b"), S("nw2b"))
            mm(BS, S("ones"), S("ec"), False, False)
        scan(S("sp_"), S("rsp"), S("b1", 0, 128), MIN)
        tt(S("thi"), S("sp_", 15, 128, 16), S("omax"), MIN)
        ts(S("tl"), S("thi"), 4095, OP.bitwise_and)
        tt(S("mk"), IND(S("tl"), S("bc8")), S("mask"), MUL)
        mm(S("b1", 128, 136), S("mk"), S("rb16"))
        cp(S("offu"), S("b1", 128, 136))
        tt(S("keep"), IND(S("yp"), S("offu")), S("z"), MIN)
        if not last:
            mm(BS, S("w2h"), S("keep"), False, True)
            seats_e()
            mm(BT, S("keep"), EYE16, False, True)
            act(S("dtr"), BT)
            mm(BD, S("dtr"), EYE)
            act(S("d"), BD)
        else:
            mm(BD, EYE16, S("keep"), False, True)
        cp(S("up"), IND(S("tl"), S("bc8")))
        mm(S("b6", 0, 128), S("up"), EYE16)
        tt(S("ohp"), S("b6", 0, 128), S("enc"), EQ)
        tt(S("comp"), S("ohp"), BW, MUL)
        for j in range(2):
            mm(S("b6", 128 + 128 * j, 256 + 128 * j), S("nbo16"), S("comp"))
        to = S("to16", 256 * t, 256 * t + 256)
        if last:
            act(S("yd_f"), BD)
            dma("A", "st_yd", T.yd[:], T.yd_f[:], [S("yd_f")], [], 2.0)
            tt(S("yc_f"), S("comp"), BC, ADD)
            dma("Y", "st_yc", T.yc[:], T.yc_f[:], [S("yc_f")], [], 2.0)
            tt(to, S("oho"), S("b6", 128, 384), MUL)
            for j in range(2):
                tt(S("yo_f", j, 256, 2), S("to16", 256 * t + 128 * j, 256 * t + 128 * j + 128),
                   S("b4", 128 * j, 128 * j + 128), ADD)
            dma("Y", "st_yo", T.yo[:], T.yo_f[:], [S("yo_f")], [], 2.0)
            return
        tt(S("n%d" % t), S("comp"), BC, ADD)
        send(t)
        tt(to, S("oho"), S("b6", 128, 384), MUL)
        mm(BO, EYE16, to, False, True)
        mm(S("b1", 256, 384), S("ones"), S("ohp"))
        act(S("kscr"), S("b1", 256, 384), 1.0, KOFF / 128, AF.Copy, S("kacc"))
        act(S("kr"), S("kacc"), 1.0, -15.5)
        act(S("kf"), S("kr"), -1.0, S("kacc"), AF.Identity)

    mms(BS, [(S("ones"), S("ec")), (S("w2b"), S("d"))])
    seats_e()
    mm(BO, EYE16, S("o16"))
    mm(BT, S("d"), EYE)
    act(S("dtr"), BT)
    for t in range(NV - 1):
        after_d(LV)
        spread()
        for s in range(2):
            index(s, S("b4", 128 * s, 128 * s + 128))
        gathers(0)
        mm(BC, EYE16, S("c%d" % t))
        index(2, BC)
        gathers(1)
        pool_card(t)
        gathers(2)
        exchange(t, LV)

    t = NV - 1
    for s in range(2):
        index(s, S("b4", 128 * s, 128 * s + 128))
    index(3, S("n0"))
    ts(S("mz"), S("mt"), 2.0, MUL)
    ts(S("dlo"), S("d"), -8.0, ADD, 1.0, MAX)
    ts(S("dhi"), S("d"), 8.0, ADD, 255.0, MIN)
    mms(S("b6", 0, 128), [(EYE, S("dhi")), (S("neye"), S("dlo"))])
    for j in range(2):
        act(S("b0", 256 * j, 256 * j + 256), S("rso"))
    pieces = [(s, lo) for s in range(3) for lo in range(0, 128, 32)]

    def gather_raw(i):
        s, lo = pieces[i]
        if i < V5RAW:
            cp(raw(s, lo, lo + 32), IND(NTAB, offs(s, lo, lo + 32)))
        else:
            act(raw(s, lo, lo + 32), IND(TAB, offs(s, lo, lo + 32)), -4.0)
    for i in range(8):
        gather_raw(i)
    mm(BC, EYE16, S("c%d" % t))
    tt(S("b5", 0, 128), S("n0"), S("c%d" % t), EQ)
    tt(S("mt"), S("b5", 0, 128), S("mz"), ADD)
    cp(S("au"), S("mt"))
    index(2, BC)
    for i in range(4):
        x, out = IND(S("tab5"), S("au", 32 * i, 32 * i + 32)), S("v5", 512 * i, 512 * i + 512)
        if i == 0:
            cp(out, x)
        else:
            act(out, x)
        scan(S("s5", 512 * i, 512 * i + 512), S("b0"), out, MAX)
    for i in range(8, 12):
        gather_raw(i)
    cp(S("vi"), S("s5", 15, W, 16))
    ts(S("vu"), S("vi"), 1, OP.bitwise_and)
    tt(S("ud"), S("vu"), S("b6", 0, 128), MUL)
    mms(BT, [(S("dlo"), EYE), (S("ud"), EYE)])
    act(S("ndtr"), BT, -1.0)
    act(S("dtr"), BT)
    mms(BD, [(EYE, S("dlo")), (EYE, S("ud"))])
    act(S("d"), BD)
    ts(S("dec"), S("d"), -1.0, ADD, 4.0, MIN)
    mm(BZ, EYE, S("dec"), True, False)
    mm(S("b7", 256, 256 + LV5), S("n4eye"), S("d", 0, LV5), False, True)
    act(S("z"), BZ)
    held = ((0, "b1"), (32, "b6"), (64, "b2"))
    for lo, bank in held:
        mm(S(bank), S("ndtr"), S("rep4", 16 * lo, 16 * lo + 512))
    for s in range(3):
        for lo, bank in held:
            tt(ybuf(s, 16 * lo, 16 * lo + 512), raw(s, lo, lo + 32), S(bank), MAX)
        clip_a(s, LV5, 128, "b3")
        scores(s)
        if s == 1:
            pool_card(t)
    exchange(t, LV5)

    n = len(ops)
    preds = [{} for _ in range(n)]
    seen, bankacc = {}, {}
    for i, (eng, call, reads, writes, dur, lat, tok) in enumerate(ops):
        def edge(j, wait, i=i):
            if j != i:
                preds[i][j] = preds[i].get(j, False) or wait
        for wr, ranges in ((False, reads), (True, writes)):
            for name, lo, hi in ranges:
                for l2, h2, j, w2 in seen.get(name, []):
                    if l2 < hi and lo < h2 and (wr or w2):
                        edge(j, (w2 and not (wr and eng == "P")) or ops[j][0] != eng or ops[j][6] is not None)
        for k in sorted({r[0] for r in reads + writes if SCRATCH[r[0]][0] == "psum"}):
            tn = bankacc.setdefault(k, [eng, [], []])
            if tn[0] != eng:
                tn[0], tn[1], tn[2] = eng, tn[2], []
            for j in tn[1]:
                edge(j, True)
            if eng == "P" and tn[2]:
                edge(tn[2][-1], False)
            tn[2].append(i)
        for name, lo, hi in writes:
            seen[name] = [e for e in seen.get(name, []) if not (lo <= e[0] and e[1] <= hi and ops[e[2]][0] != eng)]
            seen[name] = [e for e in seen[name] if not (lo == e[0] and e[1] == hi)] + [(lo, hi, i, True)]
        for name, lo, hi in reads:
            seen.setdefault(name, []).append((lo, hi, i, False))
    succs = [[] for _ in range(n)]
    for i in range(n):
        for j in preds[i]:
            succs[j].append(i)
    prio = [0.0] * n
    for i in range(n - 1, -1, -1):
        own = ops[i][4] + ops[i][5]
        best = 0.0
        for s in succs[i]:
            best = max(best, prio[s] + (own + HOP if preds[s][i] else ops[i][4]))
        prio[i] = max(best, own)
    for i in range(n):
        prio[i] += BOOST.get(ops[i][3][0][0] if ops[i][3] else "", 0.0)

    left = [len(p) for p in preds]
    est = [0.0] * n
    ready = {e: [] for e in queues}
    free = {e: 0.0 for e in queues}
    for i in range(n):
        if left[i] == 0:
            ready[ops[i][0]].append(i)
    sequence = []
    for _ in range(n):
        pick = None
        for e in queues:
            if ready[e]:
                st = max(free[e], min(est[i] for i in ready[e]))
                i = max((i for i in ready[e] if est[i] <= st + 1e-9), key=lambda i: (prio[i], -i))
                if pick is None or st < pick[0]:
                    pick = (st, e, i)
        st, e, i = pick
        ready[e].remove(i)
        sequence.append(i)
        free[e] = st + ops[i][4]
        for s in succs[i]:
            est[s] = max(est[s], free[e] + (ops[i][5] + HOP if preds[s][i] else 0.0))
            left[s] -= 1
            if left[s] == 0:
                ready[ops[s][0]].append(s)

    count = {e: 0 for e in counters}
    waited = {e: {} for e in queues}
    token = {}

    def need(e, tok):
        s, c = tok
        if waited[e].get(s, 0) < c:
            queues[e].wait_ge(T.sem[s], c)
            waited[e][s] = c

    for i in sequence:
        eng, call, reads, writes, dur, lat, tok = ops[i]
        toks = {}
        for j, w in preds[i].items():
            if w and token[j][1] > toks.get(token[j][0], 0):
                toks[token[j][0]] = token[j][1]
        for s in toks:
            need(eng, (s, toks[s]))
        if tok is None:
            count[eng] += 1
            call().then_inc(T.sem[counters[eng]], 1)
            token[i] = (counters[eng], count[eng])
        else:
            call()
            token[i] = tok
    for e in counters:
        need("G", (counters[e], count[e]))
    for s in LOADS + STORES:
        need("G", (s, 16))
    need("G", ("loc", NENG * len(ARR)))
    for s in ARR:
        need("G", (s, NENG))
